import numpy as np
import ml_dtypes


def mxq(x, axis, fmt="e4m3"):
    dtype, down = {"e4m3": (ml_dtypes.float8_e4m3fn, 7), "e5m2": (ml_dtypes.float8_e5m2, 14)}[fmt]
    v = np.moveaxis(np.asarray(x, np.float32).astype(ml_dtypes.bfloat16).astype(np.float64), axis, -1)
    blocks = v.reshape(v.shape[:-1] + (-1, 32))
    amax = np.abs(blocks).max(-1, keepdims=True)
    byte = np.maximum(np.where(amax > 0, np.frexp(amax)[1] - 1 + 127, 0) - down, 1)
    scale = np.exp2(byte - 127.0)
    codes = (blocks / scale).astype(np.float32).astype(dtype).astype(np.float64)
    return np.moveaxis((codes * scale).reshape(v.shape), -1, axis)


WIDE = False


def mx_kscale(k):
    if not WIDE:
        return np.ones(k)
    levels = np.array([10, -10, 5, -5, 0])
    if k % 512:
        return np.exp2(np.random.permutation(np.resize(levels, k // 32))).repeat(32)
    a = np.empty((k // 512, 16))
    for p in range(k // 512):
        a[p, :8] = np.random.permutation(np.resize(levels, 8))
        for g in range(8):
            far = levels[np.abs(levels - a[p, g]) >= 10]
            a[p, g + 8] = far[np.random.randint(len(far))]
    return np.exp2(a.ravel()).repeat(32)


BF16 = ml_dtypes.bfloat16


def bf(x):
    return np.asarray(x, np.float32).astype(BF16)


def f64(x):
    return np.asarray(x).astype(np.float64)


E2M1 = np.array([0.0, 0.5, 1.0, 1.5, 2.0, 3.0, 4.0, 6.0, -0.0, -0.5, -1.0, -1.5, -2.0, -3.0, -4.0, -6.0])


def pack_weight(w, fmt):
    k, n = w.shape
    w = f64(bf(w)).reshape(k // 32, 32, n)
    amax = np.abs(w).max(1)
    if fmt == "e4m3":
        byte = np.frexp(amax)[1] - 1 + 127 - 7
    else:
        mant, ex = np.frexp(amax / 6.0)
        byte = np.where(mant > 0.5, ex, ex - 1) + 127
    byte = np.clip(np.where(amax > 0, byte, 1), 1, 254)
    scaled = (w * np.exp2(127.0 - byte)[:, None, :]).reshape(k, n).astype(np.float32)
    by_word = np.ascontiguousarray(scaled.reshape(k // 512, 128, 4, n).transpose(0, 1, 3, 2))
    if fmt == "e4m3":
        words = by_word.astype(ml_dtypes.float8_e4m3fn).view(np.uint8)
    else:
        c = by_word.astype(ml_dtypes.float4_e2m1fn).view(np.uint8) & 0xF
        words = c[..., 0::2] | (c[..., 1::2] << 4)
    return np.ascontiguousarray(words), np.ascontiguousarray(byte.astype(np.uint8).reshape(k // 512, 16, n))


def unpack_weight(words, scales, fmt):
    g, p, n, _ = words.shape
    if fmt == "e4m3":
        vals = np.ascontiguousarray(words).view(ml_dtypes.float8_e4m3fn).astype(np.float64)
    else:
        nib = np.empty((g, p, n, 4), np.uint8)
        nib[..., 0::2] = words & 0xF
        nib[..., 1::2] = words >> 4
        vals = E2M1[nib]
    vals = vals * np.repeat(np.exp2(scales.astype(np.float64) - 127.0), 8, axis=1)[..., None]
    return vals.transpose(0, 1, 3, 2).reshape(g * 512, n)
def pack4(w):
    words, scales = pack_weight(w, "e2m1")
    return words.reshape(words.shape[0], 128, -1), scales


def unpack4(words, scales):
    return unpack_weight(words.reshape(words.shape[0], 128, -1, 2), scales, "e2m1")


def planes(Y):
    n, m = Y.shape
    b = f64(bf(Y)).reshape(n // 32, 32, m)
    amax = np.abs(b).max(1)
    byte = np.clip(np.where(amax > 0, np.frexp(amax)[1] - 1 + 127 - 7, 1), 1, 254)
    codes = (b * np.exp2(127.0 - byte)[:, None, :]).reshape(n, m).astype(np.float32).astype(ml_dtypes.float8_e4m3fn).view(np.uint8)
    words = codes.reshape(n // 512, 128, 4, m).transpose(0, 1, 3, 2)
    return np.ascontiguousarray(words), np.ascontiguousarray(byte.astype(np.uint8).reshape(n // 512, 16, m))


G, R, K, F, N = 4, 512, 1024, 1024, 512

def setup_inputs():
    s = mx_kscale(K)
    t = mx_kscale(F)
    x = np.random.randn(G, R, K) / s[None, None, :]
    v = np.random.randn(G, K, F) / np.sqrt(K) * s[None, :, None]
    v_words, v_scales = pack4(v.reshape(G * K, F))
    range_gain = np.exp(0.3 * np.random.randn(G, F)) * t[None, :]
    second = 1.5 * np.random.randn(G, F, N) / np.sqrt(F) / t[None, :, None]
    row_gain = np.exp(0.3 * np.random.randn(G, R))
    col_gain = np.exp(0.8 * np.random.randn(G, N))
    return {"x": bf(x), "v_words": v_words, "v_scales": v_scales,
            "range_gain": bf(range_gain), "second": bf(second),
            "row_gain": bf(row_gain), "col_gain": bf(col_gain)}

def reference(x, v_words, v_scales, range_gain, second, row_gain, col_gain):
    xq = mxq(f64(x), 2, "e4m3")
    v = unpack4(v_words, v_scales).reshape(G, K, F)
    e = xq @ v
    h = np.tanh(e) * f64(range_gain)[:, None, :]
    c = mxq(h, 2, "e4m3") @ mxq(f64(second), 1, "e4m3")
    y = np.square(c) * f64(row_gain)[:, :, None] * f64(col_gain)[:, None, :]
    Y = y.reshape(G * R, N).T
    words, scales = planes(Y)
    return y, words, scales

@@ -1,0 +1,377 @@
+from contextlib import ExitStack
+
+import concourse.mybir as mybir
+from concourse.masks import make_identity
+
+G, R, K, F, N = 4, 512, 1024, 1024, 512
+FLOPS = 2 * G * R * K * F + 2 * G * R * F * N
+
+F32 = mybir.dt.float32
+BF16 = mybir.dt.bfloat16
+I32 = mybir.dt.int32
+U32 = mybir.dt.uint32
+U8 = mybir.dt.uint8
+FP8X4 = mybir.dt.float8_e4m3fn_x4
+FP4X4 = mybir.dt.float4_e2m1fn_x4
+ACT = mybir.ActivationFunctionType
+MULT = mybir.AluOpType.mult
+
+P = 128
+TILES = G * 4
+HALF = 256
+SHARES = (0, 256, 64, 128)
+
+
+def tile_ping_pair_correlation_power_k7_kernel(
+    tc, x, v_words, v_scales, range_gain, second, row_gain, col_gain, out_0, out_1, out_2
+):
+    nc = tc.nc
+    with ExitStack() as ctx:
+        keep = ctx.enter_context(tc.tile_pool(name="keep", bufs=1))
+        work = ctx.enter_context(tc.tile_pool(name="work", bufs=2))
+        psum = ctx.enter_context(tc.psum_pool(name="psum", bufs=1))
+        ctx.enter_context(tc.manual_schedule())
+
+        ident = keep.tile([P, P], F32, name="ident")
+        make_identity(nc, ident[:])
+        warm = keep.tile([P, 8], F32, name="warm")
+        nc.vector.memset(warm[:], 0.0)
+        nc.scalar.activation(out=warm[:, 4:5], in_=warm[:, 0:1], func=ACT.Tanh)
+
+        gain_raw = keep.tile([P, 640], BF16, name="gain_raw")
+        nc.vector.memset(gain_raw[:], 0.0)
+        vs_raw = keep.tile([P, 2 * G * F], U8, name="vs_raw")
+        nc.vector.memset(vs_raw[:].bitcast(I32), 0)
+
+        x_raw, v_raw, s_raw, cg = {}, {}, {}, {}
+
+        def load_x(b):
+            for j in range(4):
+                m = 4 * b + j
+                x_raw[m] = keep.tile([P, K], BF16, name="x_raw%d" % m)
+                nc.sync.dma_start(out=x_raw[m][:], in_=x[b, P * j : P * (j + 1), :])
+
+        def load_v(b):
+            v_raw[b] = keep.tile([P, 2 * 2 * F], U8, name="v_raw%d" % b)
+            nc.sync.dma_start(
+                out=v_raw[b][:].bitcast(I32).rearrange("p (g w) -> p g w", g=2),
+                in_=v_words[2 * b : 2 * b + 2].bitcast(I32).rearrange("g p w -> p g w"),
+            )
+            for q in range(4):
+                nc.sync.dma_start(
+                    out=vs_raw[32 * q : 32 * q + 4, 2 * F * b : 2 * F * (b + 1)].bitcast(I32).rearrange("p (g w) -> p g w", g=2),
+                    in_=v_scales[2 * b : 2 * b + 2, 4 * q : 4 * q + 4, :].bitcast(I32).rearrange("g r w -> r g w"),
+                )
+
+        def load_second(b):
+            rows = second[b].rearrange("(h q t r) d -> h t q r d", h=2, t=4, r=8)
+            for h in range(2):
+                s_raw[b, h] = keep.tile([P, 4, N], BF16, name="s_raw%d_%d" % (b, h))
+                for t in range(4):
+                    nc.sync.dma_start(out=s_raw[b, h][:, t, :], in_=rows[h, t])
+
+        def load_col_gain(b):
+            cg[b] = keep.tile([P, N], BF16, name="cg%d" % b)
+            nc.sync.dma_start(out=cg[b][:], in_=col_gain[b].partition_broadcast(P))
+
+        load_x(0)
+        nc.sync.dma_start(out=gain_raw[0:8, 0:512], in_=range_gain.rearrange("b (h f) -> (b h) f", h=2))
+        nc.sync.dma_start(out=gain_raw[0:16, 512:640], in_=row_gain.rearrange("b (j r) -> (b j) r", j=4))
+        load_v(0)
+        load_second(0)
+        for b in range(1, G):
+            load_x(b)
+            load_v(b)
+            load_col_gain(b - 1)
+            load_second(b)
+        load_col_gain(G - 1)
+
+        def tr_bank():
+            return psum.tile([P, 512], F32, name="tr_bank", tag="tr", bufs=4)
+
+        def mm_bank():
+            return psum.tile([P, 512], F32, name="mm_bank", tag="mm", bufs=4)
+
+        rgain = keep.tile([P, 8, 4], F32, name="rgain")
+        wgain = keep.tile([P, TILES], F32, name="wgain")
+
+        sorted_gain = keep.tile([P, 640], F32, name="sorted_gain")
+
+        def sort_gains():
+            nc.vector.tensor_copy(
+                out=sorted_gain[:, 0:512].rearrange("p (t q r) -> p t q r", t=4, r=8),
+                in_=gain_raw[:, 0:512].rearrange("p (q t r) -> p t q r", t=4, r=8),
+            )
+            nc.vector.tensor_copy(out=sorted_gain[:, 512:640], in_=gain_raw[:, 512:640])
+
+        def transpose_gains():
+            bank = tr_bank()
+            for t in range(4):
+                nc.tensor.transpose(bank[:, P * t : P * (t + 1)], sorted_gain[:, P * t : P * (t + 1)], ident[:])
+            nc.vector.tensor_copy(out=rgain[:], in_=bank[:].rearrange("p (t a) -> p a t", t=4)[:, 0:8, :])
+            bank = tr_bank()
+            nc.tensor.transpose(bank[:, 0:P], sorted_gain[:, 512:640], ident[:])
+            nc.vector.tensor_copy(out=wgain[:], in_=bank[:, 0:TILES])
+
+        x_t, x_codes, x_scales = {}, {}, {}
+        v_sorted, vs_sorted = {}, {}
+        tanh_e, h_bf, h_codes, h_scales = {}, {}, {}, {}
+        s_il, s_codes, s_scales = {}, {}, {}
+        x_bank, e_bank, c_bank, y_bank = {}, {}, {}, {}
+        sq, y, y_bf, y_t = {}, {}, {}, {}
+        y_scales = keep.tile([P, G * R], U8, name="y_scales", align_bytes=64)
+
+        def transpose_x(m):
+            words = x_raw[m][:].bitcast(F32)
+            x_bank[m] = tr_bank()
+            for g in range(2):
+                for u in range(2):
+                    c = P * (2 * g + u)
+                    nc.tensor.transpose(x_bank[m][:, c : c + P], words[:, 256 * g + u : 256 * (g + 1) : 2], ident[:])
+
+        def copy_x(m):
+            pair, j = divmod(m, 2)
+            if j == 0:
+                x_t[pair] = work.tile([P, 2 * HALF * 4], BF16, name="x_t", bufs=3, align_bytes=64)
+            dst = x_t[pair][:].bitcast(F32).rearrange("p (g r u) -> p g r u", g=2, u=2)[:, :, P * j : P * (j + 1), :]
+            nc.scalar.copy(out=dst, in_=x_bank[m][:].rearrange("p (g u r) -> p g r u", g=2, u=2))
+
+        def quantize_x(pair):
+            b, half = divmod(pair, 2)
+            if half == 0:
+                x_codes[b] = work.tile([P, 2 * R], U32, name="x_codes", align_bytes=64)
+                x_scales[b] = work.tile([P, 2 * R], U8, name="x_scales", align_bytes=64)
+            for g in range(2):
+                c = R * g + HALF * half
+                nc.vector.quantize_mx(
+                    out=x_codes[b][:, c : c + HALF].bitcast(FP8X4),
+                    scales=x_scales[b][:, c : c + HALF],
+                    in_=x_t[pair][:, 4 * HALF * g : 4 * HALF * (g + 1)],
+                )
+
+        def sort_v(b):
+            v_sorted[b] = work.tile([P, 4 * F], U8, name="v_sorted", align_bytes=64)
+            vs_sorted[b] = work.tile([P, 2 * F], U8, name="vs_sorted", align_bytes=64)
+            nc.vector.tensor_copy(
+                out=v_sorted[b][:].bitcast(I32).rearrange("p (a t q w) -> p a t q w", a=4, t=4, q=16),
+                in_=v_raw[b][:].bitcast(I32).rearrange("p (a q t w) -> p a t q w", a=4, t=4, q=16),
+            )
+            nc.vector.tensor_copy(
+                out=vs_sorted[b][:].bitcast(I32).rearrange("p (a t q w) -> p a t q w", a=4, t=4, q=16),
+                in_=vs_raw[:, 2 * F * b : 2 * F * (b + 1)].bitcast(I32).rearrange("p (a q t w) -> p a t q w", a=4, t=4, q=16),
+            )
+
+        def filter_matmul(k):
+            b, s = divmod(k, 8)
+            e_bank[k] = mm_bank()
+            for g in range(2):
+                c = P * (8 * g + s)
+                nc.tensor.matmul_mx(
+                    out=e_bank[k][:],
+                    lhsT=v_sorted[b][:, 2 * c : 2 * (c + P)].bitcast(FP4X4),
+                    lhsT_scale=vs_sorted[b][:, c : c + P],
+                    rhs=x_codes[b][:, R * g : R * (g + 1)].bitcast(FP8X4),
+                    rhs_scale=x_scales[b][:, R * g : R * (g + 1)],
+                    start=(g == 0),
+                    stop=(g == 1),
+                )
+
+        def limit(k):
+            a, t = divmod(k, 4)
+            if t == 0:
+                tanh_e[a] = work.tile([P, 4, R], F32, name="tanh_e", bufs=3)
+            nc.scalar.activation(out=tanh_e[a][:, t, :], in_=e_bank[k][:], func=ACT.Tanh)
+
+        def apply_range_gain(n):
+            a, half = divmod(n, 2)
+            h_bf[n] = work.tile([P, HALF * 4], BF16, name="h_bf", align_bytes=64)
+            nc.vector.tensor_tensor(
+                out=h_bf[n][:].rearrange("p (c i t) -> p c t i", i=4, t=4),
+                in0=tanh_e[a][:, :, HALF * half : HALF * (half + 1)].rearrange("p t (c i) -> p c t i", i=4),
+                in1=rgain[:, a, :].unsqueeze(1).unsqueeze(3).to_broadcast([P, HALF // 4, 4, 4]),
+                op=MULT,
+            )
+
+        def quantize_h(n):
+            b, q = divmod(n, 4)
+            if q == 0:
+                h_codes[b] = work.tile([P, 2 * R], U32, name="h_codes", align_bytes=64)
+                h_scales[b] = work.tile([P, 2 * R], U8, name="h_scales", align_bytes=64)
+            cols = slice(HALF * q, HALF * (q + 1))
+            nc.vector.quantize_mx(out=h_codes[b][:, cols].bitcast(FP8X4), scales=h_scales[b][:, cols], in_=h_bf[n][:])
+
+        def interleave_second(n, first, last, copy):
+            b, q = divmod(n, 4)
+            h, half = divmod(q, 2)
+            if n not in s_il:
+                s_il[n] = work.tile([P, HALF * 4], BF16, name="s_il", align_bytes=64)
+            copy(
+                out=s_il[n][:, 4 * first : 4 * last].rearrange("p (c i t) -> p c t i", i=4, t=4),
+                in_=s_raw[b, h][:, :, HALF * half + first : HALF * half + last].rearrange("p t (c i) -> p c t i", i=4),
+            )
+
+        def quantize_second(n):
+            b, q = divmod(n, 4)
+            if q == 0:
+                s_codes[b] = work.tile([P, 2 * N], U32, name="s_codes", align_bytes=64)
+                s_scales[b] = work.tile([P, 2 * N], U8, name="s_scales", align_bytes=64)
+            cols = slice(HALF * q, HALF * (q + 1))
+            nc.vector.quantize_mx(out=s_codes[b][:, cols].bitcast(FP8X4), scales=s_scales[b][:, cols], in_=s_il[n][:])
+
+        def correlate(m):
+            b, j = divmod(m, 4)
+            c_bank[m] = mm_bank()
+            for h in range(2):
+                c = R * h + P * j
+                nc.tensor.matmul_mx(
+                    out=c_bank[m][:],
+                    lhsT=h_codes[b][:, c : c + P].bitcast(FP8X4),
+                    lhsT_scale=h_scales[b][:, c : c + P],
+                    rhs=s_codes[b][:, N * h : N * (h + 1)].bitcast(FP8X4),
+                    rhs_scale=s_scales[b][:, N * h : N * (h + 1)],
+                    start=(h == 0),
+                    stop=(h == 1),
+                )
+
+        def square(m):
+            sq[m] = work.tile([P, N], F32, name="sq", bufs=4)
+            nc.scalar.activation(out=sq[m][:], in_=c_bank[m][:], func=ACT.Square)
+
+        def weigh(m):
+            b, j = divmod(m, 4)
+            y[m] = work.tile([P, N], F32, name="y", bufs=10)
+            nc.vector.scalar_tensor_tensor(
+                out=y[m][:], in0=sq[m][:], scalar=wgain[:, m : m + 1], in1=cg[b][:], op0=MULT, op1=MULT
+            )
+            nc.sync.dma_start(out=out_0[b, P * j : P * (j + 1), :], in_=y[m][:])
+
+        def round_y(m):
+            y_bf[m] = work.tile([P, N], BF16, name="y_bf", bufs=3)
+            copy = nc.vector.tensor_copy if m >= TILES - 4 else nc.scalar.copy
+            copy(out=y_bf[m][:], in_=y[m][:])
+
+        def transpose_y(m):
+            words = y_bf[m][:].bitcast(F32)
+            y_bank[m] = tr_bank()
+            for u in range(2):
+                nc.tensor.transpose(y_bank[m][:, P * u : P * (u + 1)], words[:, u:256:2], ident[:])
+
+        def copy_y(m):
+            pair, j = divmod(m, 2)
+            if j == 0:
+                y_t[pair] = work.tile([P, HALF * 4], BF16, name="y_t", bufs=3, align_bytes=64)
+            dst = y_t[pair][:].bitcast(F32).rearrange("p (r u) -> p r u", u=2)[:, P * j : P * (j + 1), :]
+            nc.scalar.copy(out=dst, in_=y_bank[m][:, 0 : 2 * P].rearrange("p (u r) -> p r u", u=2))
+
+        def quantize_y(pair):
+            cols = slice(HALF * pair, HALF * (pair + 1))
+            y_codes = work.tile([P, HALF], U32, name="y_codes", bufs=6, align_bytes=64)
+            nc.vector.quantize_mx(out=y_codes[:].bitcast(FP8X4), scales=y_scales[:, cols], in_=y_t[pair][:])
+            nc.sync.dma_start(
+                out=out_1[0, :, cols, :].rearrange("p m t -> p (m t)").bitcast(I32), in_=y_codes[:].bitcast(I32)
+            )
+
+        def at(step, index, count):
+            if 0 <= index < count:
+                step(index)
+
+        def scalar_cols(n):
+            return SHARES[n // 4]
+
+        def interleave_on_scalar(n):
+            if scalar_cols(n) > 0:
+                interleave_second(n, 0, scalar_cols(n), nc.scalar.copy)
+
+        def interleave_on_vector(n):
+            if scalar_cols(n) < HALF:
+                interleave_second(n, scalar_cols(n), HALF, nc.vector.tensor_copy)
+
+        sort_gains()
+        for m in range(4):
+            transpose_x(m)
+            copy_x(m)
+            if m % 2 == 1:
+                quantize_x(m // 2)
+            if m == 1:
+                sort_v(0)
+        transpose_gains()
+        interleave_on_vector(0)
+
+        LAST = TILES - 2
+        for n in range(-2, LAST):
+            x_tiles = [m for m in range(4, TILES) if max(m - 7, (m - 6) // 2) == n]
+            at(filter_matmul, 2 * n + 4, 2 * TILES)
+            at(filter_matmul, 2 * n + 5, 2 * TILES)
+            at(correlate, n - 3, TILES)
+            for m in x_tiles:
+                transpose_x(m)
+            at(transpose_y, n - 6, TILES)
+            at(limit, 2 * n + 4, 2 * TILES)
+            at(limit, 2 * n + 5, 2 * TILES)
+            for m in x_tiles:
+                copy_x(m)
+            at(square, n - 3, TILES)
+            at(interleave_on_scalar, n + 3, TILES)
+            at(copy_y, n - 6, TILES)
+            at(apply_range_gain, n, TILES)
+            for pair in range(2, 2 * G):
+                if max(2 * pair - 5, pair - 2) == n:
+                    quantize_x(pair)
+            at(weigh, n - 4, TILES)
+            at(quantize_h, n, TILES)
+            at(quantize_second, n + 2, TILES)
+            at(round_y, n - 5, TILES)
+            at(interleave_on_vector, n + 3, TILES)
+            if n % 2 == 1:
+                at(quantize_y, (n - 7) // 2, 2 * G)
+            if n % 4 == 0:
+                at(sort_v, n // 4 + 1, G)
+
+        def turn_y(m):
+            transpose_y(m)
+            copy_y(m)
+
+        correlate(11)
+        square(11)
+        turn_y(8)
+        apply_range_gain(14)
+        weigh(10)
+        quantize_h(14)
+        round_y(9)
+        turn_y(9)
+        round_y(10)
+        correlate(12)
+        correlate(13)
+        square(12)
+        square(13)
+        apply_range_gain(15)
+        weigh(11)
+        quantize_h(15)
+        turn_y(10)
+        round_y(11)
+        correlate(14)
+        correlate(15)
+        square(14)
+        square(15)
+        turn_y(11)
+        quantize_y(4)
+        weigh(12)
+        weigh(13)
+        round_y(12)
+        round_y(13)
+        turn_y(12)
+        turn_y(13)
+        weigh(14)
+        quantize_y(5)
+        weigh(15)
+        round_y(14)
+        round_y(15)
+        turn_y(14)
+        turn_y(15)
+        quantize_y(6)
+        quantize_y(7)
+
+        for q in range(4):
+            nc.sync.dma_start(
+                out=out_2[0, 4 * q : 4 * q + 4, :].bitcast(I32), in_=y_scales[32 * q : 32 * q + 4, :].bitcast(I32)
+            )

@@ -19,7 +19,8 @@ MULT = mybir.AluOpType.mult
 P = 128
 TILES = G * 4
 HALF = 256
-SHARES = (0, 256, 64, 128)
+TR_BANKS = 2
+CG_BANKS = 2
 
 
 def tile_ping_pair_correlation_power_k7_kernel(
@@ -38,18 +39,19 @@ def tile_ping_pair_correlation_power_k7_kernel(
         nc.vector.memset(warm[:], 0.0)
         nc.scalar.activation(out=warm[:, 4:5], in_=warm[:, 0:1], func=ACT.Tanh)
 
-        gain_raw = keep.tile([P, 640], BF16, name="gain_raw")
-        nc.vector.memset(gain_raw[:], 0.0)
         vs_raw = keep.tile([P, 2 * G * F], U8, name="vs_raw")
-        nc.vector.memset(vs_raw[:].bitcast(I32), 0)
+        nc.vector.memset(vs_raw[:, 0 : 2 * F].bitcast(I32), 0)
+        nc.vector.memset(vs_raw[:, 2 * F :].bitcast(I32), 0)
+        gain_raw = keep.tile([P, 512], BF16, name="gain_raw")
+        sorted_gain = keep.tile([P, 512], F32, name="sorted_gain")
+        nc.gpsimd.memset(sorted_gain[:], 0.0)
 
         x_raw, v_raw, s_raw, cg = {}, {}, {}, {}
 
-        def load_x(b):
-            for j in range(4):
-                m = 4 * b + j
-                x_raw[m] = keep.tile([P, K], BF16, name="x_raw%d" % m)
-                nc.sync.dma_start(out=x_raw[m][:], in_=x[b, P * j : P * (j + 1), :])
+        def load_x(m):
+            b, j = divmod(m, 4)
+            x_raw[m] = keep.tile([P, K], BF16, name="x_raw%d" % m)
+            nc.sync.dma_start(out=x_raw[m][:], in_=x[b, P * j : P * (j + 1), :])
 
         def load_v(b):
             v_raw[b] = keep.tile([P, 2 * 2 * F], U8, name="v_raw%d" % b)
@@ -63,57 +65,66 @@ def tile_ping_pair_correlation_power_k7_kernel(
                     in_=v_scales[2 * b : 2 * b + 2, 4 * q : 4 * q + 4, :].bitcast(I32).rearrange("g r w -> r g w"),
                 )
 
-        def load_second(b):
+        def load_second(a):
+            b, h = divmod(a, 2)
             rows = second[b].rearrange("(h q t r) d -> h t q r d", h=2, t=4, r=8)
-            for h in range(2):
-                s_raw[b, h] = keep.tile([P, 4, N], BF16, name="s_raw%d_%d" % (b, h))
-                for t in range(4):
-                    nc.sync.dma_start(out=s_raw[b, h][:, t, :], in_=rows[h, t])
+            s_raw[b, h] = keep.tile([P, 4, N], BF16, name="s_raw%d" % a)
+            for t in range(4):
+                nc.sync.dma_start(out=s_raw[b, h][:, t, :], in_=rows[h, t])
 
-        def load_col_gain(b):
-            cg[b] = keep.tile([P, N], BF16, name="cg%d" % b)
-            nc.sync.dma_start(out=cg[b][:], in_=col_gain[b].partition_broadcast(P))
-
-        load_x(0)
-        nc.sync.dma_start(out=gain_raw[0:8, 0:512], in_=range_gain.rearrange("b (h f) -> (b h) f", h=2))
-        nc.sync.dma_start(out=gain_raw[0:16, 512:640], in_=row_gain.rearrange("b (j r) -> (b j) r", j=4))
+        for m in range(4):
+            load_x(m)
+        nc.sync.dma_start(out=gain_raw[0:8, :], in_=range_gain.rearrange("b (h f) -> (b h) f", h=2))
+        nc.sync.dma_start(out=gain_raw[32:48, 0:P], in_=row_gain.rearrange("b (j r) -> (b j) r", j=4))
+        nc.sync.dma_start(out=gain_raw[64:80, 0:P], in_=col_gain.rearrange("b (j d) -> (b j) d", j=4))
         load_v(0)
+        load_x(4)
         load_second(0)
+        load_x(5)
+        load_x(6)
+        load_second(1)
+        load_x(7)
         for b in range(1, G):
-            load_x(b)
             load_v(b)
-            load_col_gain(b - 1)
-            load_second(b)
-        load_col_gain(G - 1)
+            load_second(2 * b)
+            for m in range(4 * b + 4, min(4 * b + 6, TILES)):
+                load_x(m)
+            load_second(2 * b + 1)
+            for m in range(4 * b + 6, min(4 * b + 8, TILES)):
+                load_x(m)
 
         def tr_bank():
-            return psum.tile([P, 512], F32, name="tr_bank", tag="tr", bufs=4)
+            return psum.tile([P, 512], F32, name="tr_bank", tag="tr", bufs=TR_BANKS)
 
         def mm_bank():
-            return psum.tile([P, 512], F32, name="mm_bank", tag="mm", bufs=4)
+            return psum.tile([P, 512], F32, name="mm_bank", tag="mm", bufs=7 - TR_BANKS - CG_BANKS)
 
-        rgain = keep.tile([P, 8, 4], F32, name="rgain")
-        wgain = keep.tile([P, TILES], F32, name="wgain")
+        gains = psum.tile([P, 4, P], F32, name="gains")
 
-        sorted_gain = keep.tile([P, 640], F32, name="sorted_gain")
+        rg_cols = keep.tile([P, TILES], F32, name="rg_cols")
+        cg_cols = keep.tile([P, TILES], F32, name="cg_cols")
 
         def sort_gains():
             nc.vector.tensor_copy(
-                out=sorted_gain[:, 0:512].rearrange("p (t q r) -> p t q r", t=4, r=8),
-                in_=gain_raw[:, 0:512].rearrange("p (q t r) -> p t q r", t=4, r=8),
+                out=sorted_gain[0:8, :].rearrange("p (t q r) -> p t q r", t=4, r=8),
+                in_=gain_raw[0:8, :].rearrange("p (q t r) -> p t q r", t=4, r=8),
             )
-            nc.vector.tensor_copy(out=sorted_gain[:, 512:640], in_=gain_raw[:, 512:640])
+            nc.vector.tensor_copy(out=sorted_gain[32:48, 0:P], in_=gain_raw[32:48, 0:P])
+            nc.vector.tensor_copy(out=sorted_gain[64:80, 0:P], in_=gain_raw[64:80, 0:P])
 
         def transpose_gains():
-            bank = tr_bank()
             for t in range(4):
-                nc.tensor.transpose(bank[:, P * t : P * (t + 1)], sorted_gain[:, P * t : P * (t + 1)], ident[:])
-            nc.vector.tensor_copy(out=rgain[:], in_=bank[:].rearrange("p (t a) -> p a t", t=4)[:, 0:8, :])
-            bank = tr_bank()
-            nc.tensor.transpose(bank[:, 0:P], sorted_gain[:, 512:640], ident[:])
-            nc.vector.tensor_copy(out=wgain[:], in_=bank[:, 0:TILES])
+                nc.tensor.transpose(gains[:, t, :], sorted_gain[:, P * t : P * (t + 1)], ident[:])
+            nc.scalar.copy(out=rg_cols[:], in_=gains[:, 0, 32:48])
+            nc.scalar.copy(out=cg_cols[:], in_=gains[:, 0, 64:80])
 
-        x_t, x_codes, x_scales = {}, {}, {}
+        def spread_col_gain(b):
+            cg[b] = psum.tile([P, N], F32, name="cg", bufs=CG_BANKS)
+            for j in range(4):
+                column = cg_cols[:, 4 * b + j : 4 * b + j + 1]
+                nc.tensor.transpose(cg[b][:, P * j : P * (j + 1)], column.to_broadcast([P, P]), ident[:])
+
+        in_order, x_t, x_codes, x_scales = {}, {}, {}, {}
         v_sorted, vs_sorted = {}, {}
         tanh_e, h_bf, h_codes, h_scales = {}, {}, {}, {}
         s_il, s_codes, s_scales = {}, {}, {}
@@ -121,13 +132,21 @@ def tile_ping_pair_correlation_power_k7_kernel(
         sq, y, y_bf, y_t = {}, {}, {}, {}
         y_scales = keep.tile([P, G * R], U8, name="y_scales", align_bytes=64)
 
+        def sort_x(m):
+            in_order[m] = work.tile([P, K // 2], F32, name="in_order")
+            nc.vector.tensor_copy(
+                out=in_order[m][:].rearrange("p (g u k) -> p g u k", g=2, u=2),
+                in_=x_raw[m][:].bitcast(F32).rearrange("p (g k u) -> p g u k", g=2, u=2),
+            )
+
         def transpose_x(m):
             words = x_raw[m][:].bitcast(F32)
             x_bank[m] = tr_bank()
             for g in range(2):
                 for u in range(2):
                     c = P * (2 * g + u)
-                    nc.tensor.transpose(x_bank[m][:, c : c + P], words[:, 256 * g + u : 256 * (g + 1) : 2], ident[:])
+                    src = in_order[m][:, c : c + P] if m in in_order else words[:, 256 * g + u : 256 * (g + 1) : 2]
+                    nc.tensor.transpose(x_bank[m][:, c : c + P], src, ident[:])
 
         def copy_x(m):
             pair, j = divmod(m, 2)
@@ -186,9 +205,9 @@ def tile_ping_pair_correlation_power_k7_kernel(
             a, half = divmod(n, 2)
             h_bf[n] = work.tile([P, HALF * 4], BF16, name="h_bf", align_bytes=64)
             nc.vector.tensor_tensor(
-                out=h_bf[n][:].rearrange("p (c i t) -> p c t i", i=4, t=4),
-                in0=tanh_e[a][:, :, HALF * half : HALF * (half + 1)].rearrange("p t (c i) -> p c t i", i=4),
-                in1=rgain[:, a, :].unsqueeze(1).unsqueeze(3).to_broadcast([P, HALF // 4, 4, 4]),
+                out=h_bf[n][:].rearrange("p (c i t) -> p c t i", i=2, t=4),
+                in0=tanh_e[a][:, :, HALF * half : HALF * (half + 1)].rearrange("p t (c i) -> p c t i", i=2),
+                in1=gains[:, :, a : a + 1].unsqueeze(1).to_broadcast([P, HALF // 2, 4, 2]),
                 op=MULT,
             )
 
@@ -200,23 +219,42 @@ def tile_ping_pair_correlation_power_k7_kernel(
             cols = slice(HALF * q, HALF * (q + 1))
             nc.vector.quantize_mx(out=h_codes[b][:, cols].bitcast(FP8X4), scales=h_scales[b][:, cols], in_=h_bf[n][:])
 
-        def interleave_second(n, first, last, copy):
+        def second_piece(n, first, last, name, bufs):
             b, q = divmod(n, 4)
             h, half = divmod(q, 2)
-            if n not in s_il:
-                s_il[n] = work.tile([P, HALF * 4], BF16, name="s_il", align_bytes=64)
-            copy(
-                out=s_il[n][:, 4 * first : 4 * last].rearrange("p (c i t) -> p c t i", i=4, t=4),
-                in_=s_raw[b, h][:, :, HALF * half + first : HALF * half + last].rearrange("p t (c i) -> p c t i", i=4),
-            )
+            piece = work.tile([P, 4 * (last - first)], BF16, name=name, bufs=bufs, align_bytes=64)
+            s_il.setdefault(n, []).append((first, last, piece))
+            return piece[:], s_raw[b, h][:, :, HALF * half + first : HALF * half + last]
+
+        def gpsimd_cols(n):
+            return 0 if n < 3 else HALF // 2 if n < 6 else HALF
+
+        def interleave_on_gpsimd(n):
+            if gpsimd_cols(n) > 0:
+                dst, src = second_piece(n, 0, gpsimd_cols(n), "s_il_gpsimd", 1)
+                nc.gpsimd.tensor_scalar(
+                    out=dst.rearrange("p (c t) -> p c t", t=4),
+                    in0=src.rearrange("p t c -> p c t"),
+                    scalar1=1.0,
+                    scalar2=1.0,
+                    op0=MULT,
+                    op1=MULT,
+                )
+
+        def interleave_rest(n):
+            if gpsimd_cols(n) < HALF:
+                dst, src = second_piece(n, gpsimd_cols(n), HALF, "s_il", 3)
+                copy = nc.scalar.copy if n >= 3 else nc.vector.tensor_copy
+                copy(out=dst.rearrange("p (c i t) -> p c t i", i=4, t=4), in_=src.rearrange("p t (c i) -> p c t i", i=4))
 
         def quantize_second(n):
             b, q = divmod(n, 4)
             if q == 0:
                 s_codes[b] = work.tile([P, 2 * N], U32, name="s_codes", align_bytes=64)
                 s_scales[b] = work.tile([P, 2 * N], U8, name="s_scales", align_bytes=64)
-            cols = slice(HALF * q, HALF * (q + 1))
-            nc.vector.quantize_mx(out=s_codes[b][:, cols].bitcast(FP8X4), scales=s_scales[b][:, cols], in_=s_il[n][:])
+            for first, last, piece in reversed(s_il[n]):
+                cols = slice(HALF * q + first, HALF * q + last)
+                nc.vector.quantize_mx(out=s_codes[b][:, cols].bitcast(FP8X4), scales=s_scales[b][:, cols], in_=piece[:])
 
         def correlate(m):
             b, j = divmod(m, 4)
@@ -239,22 +277,25 @@ def tile_ping_pair_correlation_power_k7_kernel(
 
         def weigh(m):
             b, j = divmod(m, 4)
-            y[m] = work.tile([P, N], F32, name="y", bufs=10)
+            y[m] = work.tile([P, N], F32, name="y", bufs=9)
             nc.vector.scalar_tensor_tensor(
-                out=y[m][:], in0=sq[m][:], scalar=wgain[:, m : m + 1], in1=cg[b][:], op0=MULT, op1=MULT
+                out=y[m][:], in0=sq[m][:], scalar=rg_cols[:, m : m + 1], in1=cg[b][:], op0=MULT, op1=MULT
             )
             nc.sync.dma_start(out=out_0[b, P * j : P * (j + 1), :], in_=y[m][:])
 
         def round_y(m):
-            y_bf[m] = work.tile([P, N], BF16, name="y_bf", bufs=3)
+            y_bf[m] = work.tile([P, N], BF16, name="y_bf", bufs=4)
             copy = nc.vector.tensor_copy if m >= TILES - 4 else nc.scalar.copy
-            copy(out=y_bf[m][:], in_=y[m][:])
+            copy(
+                out=y_bf[m][:].rearrange("p (u k e) -> p u k e", u=2, e=2),
+                in_=y[m][:].rearrange("p (k u e) -> p u k e", u=2, e=2),
+            )
 
         def transpose_y(m):
             words = y_bf[m][:].bitcast(F32)
             y_bank[m] = tr_bank()
             for u in range(2):
-                nc.tensor.transpose(y_bank[m][:, P * u : P * (u + 1)], words[:, u:256:2], ident[:])
+                nc.tensor.transpose(y_bank[m][:, P * u : P * (u + 1)], words[:, P * u : P * (u + 1)], ident[:])
 
         def copy_y(m):
             pair, j = divmod(m, 2)
@@ -275,103 +316,97 @@ def tile_ping_pair_correlation_power_k7_kernel(
             if 0 <= index < count:
                 step(index)
 
-        def scalar_cols(n):
-            return SHARES[n // 4]
-
-        def interleave_on_scalar(n):
-            if scalar_cols(n) > 0:
-                interleave_second(n, 0, scalar_cols(n), nc.scalar.copy)
-
-        def interleave_on_vector(n):
-            if scalar_cols(n) < HALF:
-                interleave_second(n, scalar_cols(n), HALF, nc.vector.tensor_copy)
-
-        sort_gains()
         for m in range(4):
+            sort_x(m)
             transpose_x(m)
             copy_x(m)
-            if m % 2 == 1:
-                quantize_x(m // 2)
-            if m == 1:
-                sort_v(0)
+        sort_gains()
         transpose_gains()
-        interleave_on_vector(0)
+        transpose_x(4)
+        copy_x(4)
+        quantize_x(0)
+        sort_v(0)
+        quantize_x(1)
 
+        def store_scales(cols):
+            for q in range(4):
+                nc.sync.dma_start(
+                    out=out_2[0, 4 * q : 4 * q + 4, cols].bitcast(I32), in_=y_scales[32 * q : 32 * q + 4, cols].bitcast(I32)
+                )
+
+        interleave_rest(0)
         LAST = TILES - 2
         for n in range(-2, LAST):
-            x_tiles = [m for m in range(4, TILES) if max(m - 7, (m - 6) // 2) == n]
+            x_tiles = [m for m in range(5, TILES) if max(m - 7, -1) == n]
             at(filter_matmul, 2 * n + 4, 2 * TILES)
             at(filter_matmul, 2 * n + 5, 2 * TILES)
             at(correlate, n - 3, TILES)
-            for m in x_tiles:
-                transpose_x(m)
-            at(transpose_y, n - 6, TILES)
             at(limit, 2 * n + 4, 2 * TILES)
             at(limit, 2 * n + 5, 2 * TILES)
             for m in x_tiles:
+                transpose_x(m)
                 copy_x(m)
+            if n % 4 == 1:
+                at(spread_col_gain, n // 4, G)
+            at(transpose_y, n - 5, TILES)
             at(square, n - 3, TILES)
-            at(interleave_on_scalar, n + 3, TILES)
-            at(copy_y, n - 6, TILES)
+            at(copy_y, n - 5, TILES)
+            interleave_rest(n + 3)
+            interleave_on_gpsimd(n + 2)
             at(apply_range_gain, n, TILES)
-            for pair in range(2, 2 * G):
-                if max(2 * pair - 5, pair - 2) == n:
-                    quantize_x(pair)
             at(weigh, n - 4, TILES)
-            at(quantize_h, n, TILES)
-            at(quantize_second, n + 2, TILES)
-            at(round_y, n - 5, TILES)
-            at(interleave_on_vector, n + 3, TILES)
-            if n % 2 == 1:
-                at(quantize_y, (n - 7) // 2, 2 * G)
+            at(round_y, n - 4, TILES)
             if n % 4 == 0:
                 at(sort_v, n // 4 + 1, G)
+            if n % 2 == 1:
+                at(quantize_y, (n - 7) // 2, 2 * G)
+            if n in (0, 1):
+                quantize_x(n + 2)
+            at(quantize_h, n, TILES)
+            if n >= 2 and n % 2 == 0:
+                at(quantize_x, n // 2 + 3, 2 * G)
+            quantize_second(n + 2)
 
         def turn_y(m):
             transpose_y(m)
             copy_y(m)
 
+        store_scales(slice(0, 2 * R))
         correlate(11)
         square(11)
-        turn_y(8)
+        turn_y(9)
         apply_range_gain(14)
         weigh(10)
-        quantize_h(14)
-        round_y(9)
-        turn_y(9)
         round_y(10)
+        quantize_h(14)
         correlate(12)
         correlate(13)
         square(12)
         square(13)
+        turn_y(10)
         apply_range_gain(15)
         weigh(11)
-        quantize_h(15)
-        turn_y(10)
         round_y(11)
+        quantize_h(15)
         correlate(14)
         correlate(15)
         square(14)
         square(15)
-        turn_y(11)
-        quantize_y(4)
         weigh(12)
         weigh(13)
+        quantize_y(4)
+        turn_y(11)
         round_y(12)
         round_y(13)
         turn_y(12)
         turn_y(13)
         weigh(14)
-        quantize_y(5)
         weigh(15)
         round_y(14)
+        quantize_y(5)
         round_y(15)
         turn_y(14)
         turn_y(15)
         quantize_y(6)
         quantize_y(7)
-
-        for q in range(4):
-            nc.sync.dma_start(
-                out=out_2[0, 4 * q : 4 * q + 4, :].bitcast(I32), in_=y_scales[32 * q : 32 * q + 4, :].bitcast(I32)
-            )
+        store_scales(slice(2 * R, 4 * R))

@@ -17,10 +17,9 @@ ACT = mybir.ActivationFunctionType
 MULT = mybir.AluOpType.mult
 
 P = 128
-TILES = G * 4
+PASSES = 2 * G
+TILES = 4 * G
 HALF = 256
-TR_BANKS = 2
-CG_BANKS = 2
 
 
 def tile_ping_pair_correlation_power_k7_kernel(
@@ -39,26 +38,29 @@ def tile_ping_pair_correlation_power_k7_kernel(
         nc.vector.memset(warm[:], 0.0)
         nc.scalar.activation(out=warm[:, 4:5], in_=warm[:, 0:1], func=ACT.Tanh)
 
-        vs_raw = keep.tile([P, 2 * G * F], U8, name="vs_raw")
+        vs_raw = keep.tile([P, PASSES * F], U8, name="vs_raw")
         nc.vector.memset(vs_raw[:, 0 : 2 * F].bitcast(I32), 0)
         nc.vector.memset(vs_raw[:, 2 * F :].bitcast(I32), 0)
         gain_raw = keep.tile([P, 512], BF16, name="gain_raw")
         sorted_gain = keep.tile([P, 512], F32, name="sorted_gain")
         nc.gpsimd.memset(sorted_gain[:], 0.0)
 
-        x_raw, v_raw, s_raw, cg = {}, {}, {}, {}
+        x_raw, v_raw, s_raw = {}, {}, {}
 
         def load_x(m):
-            b, j = divmod(m, 4)
-            x_raw[m] = keep.tile([P, K], BF16, name="x_raw%d" % m)
-            nc.sync.dma_start(out=x_raw[m][:], in_=x[b, P * j : P * (j + 1), :])
+            b, g, half = m // 4, m // 2 % 2, m % 2
+            x_raw[m] = keep.tile([P, 2, 512], BF16, name="x_raw%d" % m)
+            rows = x[b, HALF * half : HALF * (half + 1), 512 * g : 512 * (g + 1)]
+            nc.sync.dma_start(out=x_raw[m][:], in_=rows.rearrange("(j p) k -> p j k", j=2))
 
-        def load_v(b):
-            v_raw[b] = keep.tile([P, 2 * 2 * F], U8, name="v_raw%d" % b)
+        def load_v_words(first, last):
+            v_raw[first] = keep.tile([P, (last - first) * 2 * F], U8, name="v_raw%d" % first)
             nc.sync.dma_start(
-                out=v_raw[b][:].bitcast(I32).rearrange("p (g w) -> p g w", g=2),
-                in_=v_words[2 * b : 2 * b + 2].bitcast(I32).rearrange("g p w -> p g w"),
+                out=v_raw[first][:].bitcast(I32).rearrange("p (g w) -> p g w", g=last - first),
+                in_=v_words[first:last].bitcast(I32).rearrange("g p w -> p g w"),
             )
+
+        def load_v_scales(b):
             for q in range(4):
                 nc.sync.dma_start(
                     out=vs_raw[32 * q : 32 * q + 4, 2 * F * b : 2 * F * (b + 1)].bitcast(I32).rearrange("p (g w) -> p g w", g=2),
@@ -68,41 +70,44 @@ def tile_ping_pair_correlation_power_k7_kernel(
         def load_second(a):
             b, h = divmod(a, 2)
             rows = second[b].rearrange("(h q t r) d -> h t q r d", h=2, t=4, r=8)
-            s_raw[b, h] = keep.tile([P, 4, N], BF16, name="s_raw%d" % a)
+            s_raw[a] = keep.tile([P, 4, N], BF16, name="s_raw%d" % a)
             for t in range(4):
-                nc.sync.dma_start(out=s_raw[b, h][:, t, :], in_=rows[h, t])
+                nc.sync.dma_start(out=s_raw[a][:, t, :], in_=rows[h, t])
 
-        for m in range(4):
-            load_x(m)
+        load_x(0)
+        load_x(1)
+        load_v_words(0, 1)
+        load_x(2)
+        load_x(3)
+        load_v_scales(0)
+        load_v_words(1, 2)
         nc.sync.dma_start(out=gain_raw[0:8, :], in_=range_gain.rearrange("b (h f) -> (b h) f", h=2))
         nc.sync.dma_start(out=gain_raw[32:48, 0:P], in_=row_gain.rearrange("b (j r) -> (b j) r", j=4))
         nc.sync.dma_start(out=gain_raw[64:80, 0:P], in_=col_gain.rearrange("b (j d) -> (b j) d", j=4))
-        load_v(0)
-        load_x(4)
         load_second(0)
+        load_x(4)
         load_x(5)
-        load_x(6)
         load_second(1)
+        load_x(6)
         load_x(7)
         for b in range(1, G):
-            load_v(b)
-            load_second(2 * b)
-            for m in range(4 * b + 4, min(4 * b + 6, TILES)):
-                load_x(m)
-            load_second(2 * b + 1)
-            for m in range(4 * b + 6, min(4 * b + 8, TILES)):
-                load_x(m)
+            load_v_words(2 * b, 2 * b + 2)
+            load_v_scales(b)
+            for h in range(2):
+                for m in range(4 * b + 4 + 2 * h, min(4 * b + 6 + 2 * h, TILES)):
+                    load_x(m)
+                load_second(2 * b + h)
 
         def tr_bank():
-            return psum.tile([P, 512], F32, name="tr_bank", tag="tr", bufs=TR_BANKS)
+            return psum.tile([P, 512], F32, name="tr_bank", tag="tr", bufs=2)
 
         def mm_bank():
-            return psum.tile([P, 512], F32, name="mm_bank", tag="mm", bufs=7 - TR_BANKS - CG_BANKS)
+            return psum.tile([P, 512], F32, name="mm_bank", tag="mm", bufs=3)
 
         gains = psum.tile([P, 4, P], F32, name="gains")
-
         rg_cols = keep.tile([P, TILES], F32, name="rg_cols")
         cg_cols = keep.tile([P, TILES], F32, name="cg_cols")
+        cg = {}
 
         def sort_gains():
             nc.vector.tensor_copy(
@@ -119,81 +124,78 @@ def tile_ping_pair_correlation_power_k7_kernel(
             nc.scalar.copy(out=cg_cols[:], in_=gains[:, 0, 64:80])
 
         def spread_col_gain(b):
-            cg[b] = psum.tile([P, N], F32, name="cg", bufs=CG_BANKS)
+            cg[b] = psum.tile([P, N], F32, name="cg", bufs=2)
             for j in range(4):
                 column = cg_cols[:, 4 * b + j : 4 * b + j + 1]
                 nc.tensor.transpose(cg[b][:, P * j : P * (j + 1)], column.to_broadcast([P, P]), ident[:])
 
         in_order, x_t, x_codes, x_scales = {}, {}, {}, {}
         v_sorted, vs_sorted = {}, {}
-        tanh_e, h_bf, h_codes, h_scales = {}, {}, {}, {}
+        e_bank, tanh_e, h_bf, h_codes, h_scales = {}, {}, {}, {}, {}
         s_il, s_codes, s_scales = {}, {}, {}
-        x_bank, e_bank, c_bank, y_bank = {}, {}, {}, {}
-        sq, y, y_bf, y_t = {}, {}, {}, {}
+        c_bank, sq, y, y_bf, y_t = {}, {}, {}, {}, {}
         y_scales = keep.tile([P, G * R], U8, name="y_scales", align_bytes=64)
 
         def sort_x(m):
-            in_order[m] = work.tile([P, K // 2], F32, name="in_order")
+            in_order[m] = work.tile([P, 512], F32, name="in_order")
             nc.vector.tensor_copy(
-                out=in_order[m][:].rearrange("p (g u k) -> p g u k", g=2, u=2),
-                in_=x_raw[m][:].bitcast(F32).rearrange("p (g k u) -> p g u k", g=2, u=2),
+                out=in_order[m][:].rearrange("p (j u k) -> p j u k", j=2, u=2),
+                in_=x_raw[m][:].bitcast(F32).rearrange("p j (k u) -> p j u k", u=2),
             )
 
-        def transpose_x(m):
+        def turn_x(m):
+            i, half = divmod(m, 2)
             words = x_raw[m][:].bitcast(F32)
-            x_bank[m] = tr_bank()
-            for g in range(2):
+            bank = tr_bank()
+            for j in range(2):
                 for u in range(2):
-                    c = P * (2 * g + u)
-                    src = in_order[m][:, c : c + P] if m in in_order else words[:, 256 * g + u : 256 * (g + 1) : 2]
-                    nc.tensor.transpose(x_bank[m][:, c : c + P], src, ident[:])
-
-        def copy_x(m):
-            pair, j = divmod(m, 2)
-            if j == 0:
-                x_t[pair] = work.tile([P, 2 * HALF * 4], BF16, name="x_t", bufs=3, align_bytes=64)
-            dst = x_t[pair][:].bitcast(F32).rearrange("p (g r u) -> p g r u", g=2, u=2)[:, :, P * j : P * (j + 1), :]
-            nc.scalar.copy(out=dst, in_=x_bank[m][:].rearrange("p (g u r) -> p g r u", g=2, u=2))
-
-        def quantize_x(pair):
-            b, half = divmod(pair, 2)
+                    c = P * (2 * j + u)
+                    src = in_order[m][:, c : c + P] if m in in_order else words[:, j, u:256:2]
+                    nc.tensor.transpose(bank[:, c : c + P], src, ident[:])
             if half == 0:
+                x_t[i] = work.tile([P, R * 4], BF16, name="x_t", bufs=3, align_bytes=64)
+            dst = x_t[i][:, 4 * HALF * half : 4 * HALF * (half + 1)].bitcast(F32)
+            nc.scalar.copy(
+                out=dst.rearrange("p (j r u) -> p j r u", j=2, u=2), in_=bank[:].rearrange("p (j u r) -> p j r u", j=2, u=2)
+            )
+
+        def quantize_x(i):
+            b, g = divmod(i, 2)
+            if g == 0:
                 x_codes[b] = work.tile([P, 2 * R], U32, name="x_codes", align_bytes=64)
                 x_scales[b] = work.tile([P, 2 * R], U8, name="x_scales", align_bytes=64)
-            for g in range(2):
-                c = R * g + HALF * half
-                nc.vector.quantize_mx(
-                    out=x_codes[b][:, c : c + HALF].bitcast(FP8X4),
-                    scales=x_scales[b][:, c : c + HALF],
-                    in_=x_t[pair][:, 4 * HALF * g : 4 * HALF * (g + 1)],
+            cols = slice(R * g, R * (g + 1))
+            nc.vector.quantize_mx(out=x_codes[b][:, cols].bitcast(FP8X4), scales=x_scales[b][:, cols], in_=x_t[i][:])
+
+        def sort_v(first, last):
+            b, g = divmod(first, 2)
+            if g == 0:
+                v_sorted[b] = work.tile([P, 4 * F], U8, name="v_sorted", align_bytes=64)
+                vs_sorted[b] = work.tile([P, 2 * F], U8, name="vs_sorted", align_bytes=64)
+            count = last - first
+            for dst, src in (
+                (v_sorted[b][:, 2 * F * g : 2 * F * (g + count)], v_raw[first][:]),
+                (vs_sorted[b][:, F * g : F * (g + count)], vs_raw[:, F * first : F * last]),
+            ):
+                nc.vector.tensor_copy(
+                    out=dst.bitcast(I32).rearrange("p (a t q w) -> p a t q w", a=2 * count, t=4, q=16),
+                    in_=src.bitcast(I32).rearrange("p (a q t w) -> p a t q w", a=2 * count, t=4, q=16),
                 )
 
-        def sort_v(b):
-            v_sorted[b] = work.tile([P, 4 * F], U8, name="v_sorted", align_bytes=64)
-            vs_sorted[b] = work.tile([P, 2 * F], U8, name="vs_sorted", align_bytes=64)
-            nc.vector.tensor_copy(
-                out=v_sorted[b][:].bitcast(I32).rearrange("p (a t q w) -> p a t q w", a=4, t=4, q=16),
-                in_=v_raw[b][:].bitcast(I32).rearrange("p (a q t w) -> p a t q w", a=4, t=4, q=16),
-            )
-            nc.vector.tensor_copy(
-                out=vs_sorted[b][:].bitcast(I32).rearrange("p (a t q w) -> p a t q w", a=4, t=4, q=16),
-                in_=vs_raw[:, 2 * F * b : 2 * F * (b + 1)].bitcast(I32).rearrange("p (a q t w) -> p a t q w", a=4, t=4, q=16),
-            )
-
-        def filter_matmul(k):
+        def filter_pass(k, g):
             b, s = divmod(k, 8)
-            e_bank[k] = mm_bank()
-            for g in range(2):
-                c = P * (8 * g + s)
-                nc.tensor.matmul_mx(
-                    out=e_bank[k][:],
-                    lhsT=v_sorted[b][:, 2 * c : 2 * (c + P)].bitcast(FP4X4),
-                    lhsT_scale=vs_sorted[b][:, c : c + P],
-                    rhs=x_codes[b][:, R * g : R * (g + 1)].bitcast(FP8X4),
-                    rhs_scale=x_scales[b][:, R * g : R * (g + 1)],
-                    start=(g == 0),
-                    stop=(g == 1),
-                )
+            if g == 0:
+                e_bank[k] = mm_bank()
+            c = P * (8 * g + s)
+            nc.tensor.matmul_mx(
+                out=e_bank[k][:],
+                lhsT=v_sorted[b][:, 2 * c : 2 * (c + P)].bitcast(FP4X4),
+                lhsT_scale=vs_sorted[b][:, c : c + P],
+                rhs=x_codes[b][:, R * g : R * (g + 1)].bitcast(FP8X4),
+                rhs_scale=x_scales[b][:, R * g : R * (g + 1)],
+                start=(g == 0),
+                stop=(g == 1),
+            )
 
         def limit(k):
             a, t = divmod(k, 4)
@@ -201,68 +203,66 @@ def tile_ping_pair_correlation_power_k7_kernel(
                 tanh_e[a] = work.tile([P, 4, R], F32, name="tanh_e", bufs=3)
             nc.scalar.activation(out=tanh_e[a][:, t, :], in_=e_bank[k][:], func=ACT.Tanh)
 
-        def apply_range_gain(n):
-            a, half = divmod(n, 2)
-            h_bf[n] = work.tile([P, HALF * 4], BF16, name="h_bf", align_bytes=64)
+        def filter_and_limit(k):
+            filter_pass(k, 0)
+            filter_pass(k, 1)
+            limit(k)
+
+        def apply_range_gain(a, first, last):
+            if first == 0:
+                h_bf[a] = work.tile([P, R * 4], BF16, name="h_bf", align_bytes=64)
             nc.vector.tensor_tensor(
-                out=h_bf[n][:].rearrange("p (c i t) -> p c t i", i=2, t=4),
-                in0=tanh_e[a][:, :, HALF * half : HALF * (half + 1)].rearrange("p t (c i) -> p c t i", i=2),
-                in1=gains[:, :, a : a + 1].unsqueeze(1).to_broadcast([P, HALF // 2, 4, 2]),
+                out=h_bf[a][:, 4 * first : 4 * last].rearrange("p (c i t) -> p c t i", i=2, t=4),
+                in0=tanh_e[a][:, :, first:last].rearrange("p t (c i) -> p c t i", i=2),
+                in1=gains[:, :, a : a + 1].unsqueeze(1).to_broadcast([P, (last - first) // 2, 4, 2]),
                 op=MULT,
             )
 
-        def quantize_h(n):
-            b, q = divmod(n, 4)
-            if q == 0:
+        def quantize_h(a, first, last):
+            b, h = divmod(a, 2)
+            if h == 0:
                 h_codes[b] = work.tile([P, 2 * R], U32, name="h_codes", align_bytes=64)
                 h_scales[b] = work.tile([P, 2 * R], U8, name="h_scales", align_bytes=64)
-            cols = slice(HALF * q, HALF * (q + 1))
-            nc.vector.quantize_mx(out=h_codes[b][:, cols].bitcast(FP8X4), scales=h_scales[b][:, cols], in_=h_bf[n][:])
+            cols = slice(R * h + first, R * h + last)
+            nc.vector.quantize_mx(
+                out=h_codes[b][:, cols].bitcast(FP8X4), scales=h_scales[b][:, cols], in_=h_bf[a][:, 4 * first : 4 * last]
+            )
 
-        def second_piece(n, first, last, name, bufs):
-            b, q = divmod(n, 4)
-            h, half = divmod(q, 2)
+        def second_piece(a, first, last, name, bufs):
             piece = work.tile([P, 4 * (last - first)], BF16, name=name, bufs=bufs, align_bytes=64)
-            s_il.setdefault(n, []).append((first, last, piece))
-            return piece[:], s_raw[b, h][:, :, HALF * half + first : HALF * half + last]
+            s_il[a, first] = piece
+            return piece[:], s_raw[a][:, :, first:last]
 
-        def gpsimd_cols(n):
-            return 0 if n < 3 else HALF // 2 if n < 6 else HALF
+        def interleave_on_gpsimd(a, first, last):
+            dst, src = second_piece(a, first, last, "s_il_gpsimd", 1)
+            nc.gpsimd.tensor_scalar(
+                out=dst.rearrange("p (c t) -> p c t", t=4),
+                in0=src.rearrange("p t c -> p c t"),
+                scalar1=1.0,
+                scalar2=1.0,
+                op0=MULT,
+                op1=MULT,
+            )
 
-        def interleave_on_gpsimd(n):
-            if gpsimd_cols(n) > 0:
-                dst, src = second_piece(n, 0, gpsimd_cols(n), "s_il_gpsimd", 1)
-                nc.gpsimd.tensor_scalar(
-                    out=dst.rearrange("p (c t) -> p c t", t=4),
-                    in0=src.rearrange("p t c -> p c t"),
-                    scalar1=1.0,
-                    scalar2=1.0,
-                    op0=MULT,
-                    op1=MULT,
-                )
+        def interleave_by_copy(a, first, last, copy):
+            dst, src = second_piece(a, first, last, "s_il", 3)
+            copy(out=dst.rearrange("p (c i t) -> p c t i", i=4, t=4), in_=src.rearrange("p t (c i) -> p c t i", i=4))
 
-        def interleave_rest(n):
-            if gpsimd_cols(n) < HALF:
-                dst, src = second_piece(n, gpsimd_cols(n), HALF, "s_il", 3)
-                copy = nc.scalar.copy if n >= 3 else nc.vector.tensor_copy
-                copy(out=dst.rearrange("p (c i t) -> p c t i", i=4, t=4), in_=src.rearrange("p t (c i) -> p c t i", i=4))
-
-        def quantize_second(n):
-            b, q = divmod(n, 4)
-            if q == 0:
+        def quantize_second(a, first, last):
+            b, h = divmod(a, 2)
+            if b not in s_codes:
                 s_codes[b] = work.tile([P, 2 * N], U32, name="s_codes", align_bytes=64)
                 s_scales[b] = work.tile([P, 2 * N], U8, name="s_scales", align_bytes=64)
-            for first, last, piece in reversed(s_il[n]):
-                cols = slice(HALF * q + first, HALF * q + last)
-                nc.vector.quantize_mx(out=s_codes[b][:, cols].bitcast(FP8X4), scales=s_scales[b][:, cols], in_=piece[:])
+            cols = slice(N * h + first, N * h + last)
+            nc.vector.quantize_mx(out=s_codes[b][:, cols].bitcast(FP8X4), scales=s_scales[b][:, cols], in_=s_il[a, first][:])
 
-        def correlate(m):
+        def correlate_and_square(m):
             b, j = divmod(m, 4)
-            c_bank[m] = mm_bank()
+            bank = mm_bank()
             for h in range(2):
                 c = R * h + P * j
                 nc.tensor.matmul_mx(
-                    out=c_bank[m][:],
+                    out=bank[:],
                     lhsT=h_codes[b][:, c : c + P].bitcast(FP8X4),
                     lhsT_scale=h_scales[b][:, c : c + P],
                     rhs=s_codes[b][:, N * h : N * (h + 1)].bitcast(FP8X4),
@@ -270,63 +270,77 @@ def tile_ping_pair_correlation_power_k7_kernel(
                     start=(h == 0),
                     stop=(h == 1),
                 )
-
-        def square(m):
-            sq[m] = work.tile([P, N], F32, name="sq", bufs=4)
-            nc.scalar.activation(out=sq[m][:], in_=c_bank[m][:], func=ACT.Square)
+            sq[m] = work.tile([P, N], F32, name="sq", bufs=5)
+            nc.scalar.activation(out=sq[m][:], in_=bank[:], func=ACT.Square)
 
         def weigh(m):
-            b, j = divmod(m, 4)
-            y[m] = work.tile([P, N], F32, name="y", bufs=9)
-            nc.vector.scalar_tensor_tensor(
-                out=y[m][:], in0=sq[m][:], scalar=rg_cols[:, m : m + 1], in1=cg[b][:], op0=MULT, op1=MULT
-            )
-            nc.sync.dma_start(out=out_0[b, P * j : P * (j + 1), :], in_=y[m][:])
-
-        def round_y(m):
-            y_bf[m] = work.tile([P, N], BF16, name="y_bf", bufs=4)
-            copy = nc.vector.tensor_copy if m >= TILES - 4 else nc.scalar.copy
-            copy(
-                out=y_bf[m][:].rearrange("p (u k e) -> p u k e", u=2, e=2),
-                in_=y[m][:].rearrange("p (k u e) -> p u k e", u=2, e=2),
-            )
-
-        def transpose_y(m):
-            words = y_bf[m][:].bitcast(F32)
-            y_bank[m] = tr_bank()
-            for u in range(2):
-                nc.tensor.transpose(y_bank[m][:, P * u : P * (u + 1)], words[:, P * u : P * (u + 1)], ident[:])
-
-        def copy_y(m):
             pair, j = divmod(m, 2)
             if j == 0:
-                y_t[pair] = work.tile([P, HALF * 4], BF16, name="y_t", bufs=3, align_bytes=64)
-            dst = y_t[pair][:].bitcast(F32).rearrange("p (r u) -> p r u", u=2)[:, P * j : P * (j + 1), :]
-            nc.scalar.copy(out=dst, in_=y_bank[m][:, 0 : 2 * P].rearrange("p (u r) -> p r u", u=2))
+                y[pair] = work.tile([P, 2 * N], F32, name="y", bufs=3)
+            nc.vector.scalar_tensor_tensor(
+                out=y[pair][:, N * j : N * (j + 1)],
+                in0=sq[m][:],
+                scalar=rg_cols[:, m : m + 1],
+                in1=cg[m // 4][:],
+                op0=MULT,
+                op1=MULT,
+            )
+
+        def store_y(first, last):
+            pair, j = divmod(first, 2)
+            b, r0 = divmod(P * first, R)
+            count = last - first
+            nc.sync.dma_start(
+                out=out_0[b, r0 : r0 + P * count, :].rearrange("(j p) d -> p j d", p=P),
+                in_=y[pair][:, N * j : N * (j + count)].rearrange("p (j d) -> p j d", d=N),
+            )
+
+        def round_y(first, last, copy):
+            pair, j = divmod(first, 2)
+            if j == 0:
+                y_bf[pair] = work.tile([P, 2 * N], BF16, name="y_bf", bufs=3)
+            cols = slice(N * j, N * (j + last - first))
+            copy(
+                out=y_bf[pair][:, cols].rearrange("p (j u k e) -> p j u k e", u=2, k=P, e=2),
+                in_=y[pair][:, cols].rearrange("p (j k u e) -> p j u k e", u=2, k=P, e=2),
+            )
+
+        def round_y_on_gpsimd(m):
+            pair, j = divmod(m, 2)
+            if j == 0:
+                y_bf[pair] = work.tile([P, 2 * N], BF16, name="y_bf", bufs=3)
+            cols = slice(N * j, N * (j + 1))
+            nc.gpsimd.tensor_scalar(
+                out=y_bf[pair][:, cols].rearrange("p (u k e) -> p u k e", u=2, e=2),
+                in0=y[pair][:, cols].rearrange("p (k u e) -> p u k e", u=2, e=2),
+                scalar1=1.0,
+                scalar2=1.0,
+                op0=MULT,
+                op1=MULT,
+            )
+
+        def turn_y(first, last, copy):
+            pair, j = divmod(first, 2)
+            count = last - first
+            words = y_bf[pair][:].bitcast(F32)
+            bank = tr_bank()
+            for c in range(0, 2 * P * count, P):
+                nc.tensor.transpose(bank[:, c : c + P], words[:, 2 * P * j + c : 2 * P * j + c + P], ident[:])
+            if j == 0:
+                y_t[pair] = work.tile([P, HALF * 4], BF16, name="y_t", align_bytes=64)
+            dst = y_t[pair][:, 4 * P * j : 4 * P * (j + count)].bitcast(F32)
+            copy(
+                out=dst.rearrange("p (j r u) -> p j r u", r=P, u=2),
+                in_=bank[:, 0 : 2 * P * count].rearrange("p (j u r) -> p j r u", r=P, u=2),
+            )
 
         def quantize_y(pair):
             cols = slice(HALF * pair, HALF * (pair + 1))
-            y_codes = work.tile([P, HALF], U32, name="y_codes", bufs=6, align_bytes=64)
+            y_codes = work.tile([P, HALF], U32, name="y_codes", bufs=4, align_bytes=64)
             nc.vector.quantize_mx(out=y_codes[:].bitcast(FP8X4), scales=y_scales[:, cols], in_=y_t[pair][:])
             nc.sync.dma_start(
                 out=out_1[0, :, cols, :].rearrange("p m t -> p (m t)").bitcast(I32), in_=y_codes[:].bitcast(I32)
             )
-
-        def at(step, index, count):
-            if 0 <= index < count:
-                step(index)
-
-        for m in range(4):
-            sort_x(m)
-            transpose_x(m)
-            copy_x(m)
-        sort_gains()
-        transpose_gains()
-        transpose_x(4)
-        copy_x(4)
-        quantize_x(0)
-        sort_v(0)
-        quantize_x(1)
 
         def store_scales(cols):
             for q in range(4):
@@ -334,79 +348,102 @@ def tile_ping_pair_correlation_power_k7_kernel(
                     out=out_2[0, 4 * q : 4 * q + 4, cols].bitcast(I32), in_=y_scales[32 * q : 32 * q + 4, cols].bitcast(I32)
                 )
 
-        interleave_rest(0)
-        LAST = TILES - 2
-        for n in range(-2, LAST):
-            x_tiles = [m for m in range(5, TILES) if max(m - 7, -1) == n]
-            at(filter_matmul, 2 * n + 4, 2 * TILES)
-            at(filter_matmul, 2 * n + 5, 2 * TILES)
-            at(correlate, n - 3, TILES)
-            at(limit, 2 * n + 4, 2 * TILES)
-            at(limit, 2 * n + 5, 2 * TILES)
-            for m in x_tiles:
-                transpose_x(m)
-                copy_x(m)
-            if n % 4 == 1:
-                at(spread_col_gain, n // 4, G)
-            at(transpose_y, n - 5, TILES)
-            at(square, n - 3, TILES)
-            at(copy_y, n - 5, TILES)
-            interleave_rest(n + 3)
-            interleave_on_gpsimd(n + 2)
-            at(apply_range_gain, n, TILES)
-            at(weigh, n - 4, TILES)
-            at(round_y, n - 4, TILES)
-            if n % 4 == 0:
-                at(sort_v, n // 4 + 1, G)
-            if n % 2 == 1:
-                at(quantize_y, (n - 7) // 2, 2 * G)
-            if n in (0, 1):
-                quantize_x(n + 2)
-            at(quantize_h, n, TILES)
-            if n >= 2 and n % 2 == 0:
-                at(quantize_x, n // 2 + 3, 2 * G)
-            quantize_second(n + 2)
+        for m in range(4):
+            sort_x(m)
+            turn_x(m)
+        quantize_x(0)
+        sort_v(0, 1)
+        sort_v(1, 2)
+        quantize_x(1)
+        for g in range(2):
+            for k in range(3):
+                filter_pass(k, g)
+        for k in range(3):
+            limit(k)
+        filter_and_limit(3)
+        sort_gains()
+        transpose_gains()
+        turn_x(4)
+        turn_x(5)
+        interleave_by_copy(0, 0, HALF, nc.vector.tensor_copy)
+        interleave_by_copy(0, HALF, N, nc.vector.tensor_copy)
+        quantize_second(0, 0, HALF)
+        quantize_second(0, HALF, N)
 
-        def turn_y(m):
-            transpose_y(m)
-            copy_y(m)
+        for a in range(PASSES - 1):
+            gpsimd_first = HALF if a < 2 else 0
+            if a >= 2:
+                correlate_and_square(2 * a - 4)
+                correlate_and_square(2 * a - 3)
+            x_units = ([6, 7], [8, 9, 10, 11])[a] if a < 2 else [m for m in (2 * a + 8, 2 * a + 9) if m < TILES]
+            early = 2 if a < 2 else 1
+            filter_and_limit(4 * a + 4)
+            filter_and_limit(4 * a + 5)
+            for m in x_units[:early]:
+                turn_x(m)
+            if a % 2 == 1:
+                spread_col_gain(a // 2)
+            filter_and_limit(4 * a + 6)
+            filter_and_limit(4 * a + 7)
+            for m in x_units[early:]:
+                turn_x(m)
+            if a == 0:
+                interleave_by_copy(1, 0, HALF, nc.scalar.copy)
+            if a >= 3:
+                turn_y(2 * a - 6, 2 * a - 4, nc.scalar.copy)
 
+            interleave_on_gpsimd(a + 1, gpsimd_first, N)
+            apply_range_gain(a, 0, R)
+            if a >= 2:
+                weigh(2 * a - 4)
+                weigh(2 * a - 3)
+                store_y(2 * a - 4, 2 * a - 2)
+                round_y(2 * a - 4, 2 * a - 2, nc.scalar.copy)
+            if a == 0:
+                quantize_x(2)
+            if a == 1:
+                interleave_by_copy(2, 0, HALF, nc.vector.tensor_copy)
+                quantize_second(1, 0, HALF)
+            if a % 2 == 0 and a + 2 < PASSES:
+                sort_v(a + 2, a + 4)
+            if a + 3 < PASSES and a != 1:
+                quantize_x(a + 3)
+            quantize_h(a, 0, R)
+            if a == 1:
+                quantize_second(2, 0, HALF)
+                quantize_x(4)
+            if a >= 4:
+                quantize_y(a - 4)
+            quantize_second(a + 1, gpsimd_first, N)
+
+        spread_col_gain(G - 1)
+        correlate_and_square(10)
+        correlate_and_square(11)
+        turn_y(8, 10, nc.scalar.copy)
+        apply_range_gain(7, 0, HALF)
+        quantize_y(3)
         store_scales(slice(0, 2 * R))
-        correlate(11)
-        square(11)
-        turn_y(9)
-        apply_range_gain(14)
-        weigh(10)
-        round_y(10)
-        quantize_h(14)
-        correlate(12)
-        correlate(13)
-        square(12)
-        square(13)
-        turn_y(10)
-        apply_range_gain(15)
-        weigh(11)
-        round_y(11)
-        quantize_h(15)
-        correlate(14)
-        correlate(15)
-        square(14)
-        square(15)
-        weigh(12)
-        weigh(13)
+        quantize_h(7, 0, HALF)
+        correlate_and_square(12)
+        correlate_and_square(13)
+        apply_range_gain(7, HALF, R)
         quantize_y(4)
-        turn_y(11)
-        round_y(12)
-        round_y(13)
-        turn_y(12)
-        turn_y(13)
-        weigh(14)
-        weigh(15)
-        round_y(14)
+        quantize_h(7, HALF, R)
+        weigh(10)
+        correlate_and_square(14)
+        correlate_and_square(15)
+        for m in range(11, TILES):
+            weigh(m)
+            if m % 2 == 1 or m == TILES - 2:
+                store_y(m - 1 if m < TILES - 2 else m, m + 1)
+            if m - 1 < TILES - 2:
+                round_y_on_gpsimd(m - 1)
+        turn_y(10, 12, nc.scalar.copy)
+        round_y(14, 15, nc.scalar.copy)
         quantize_y(5)
-        round_y(15)
-        turn_y(14)
-        turn_y(15)
+        round_y(15, 16, nc.vector.tensor_copy)
+        turn_y(12, 14, nc.vector.tensor_copy)
+        turn_y(14, 16, nc.scalar.copy)
         quantize_y(6)
         quantize_y(7)
         store_scales(slice(2 * R, 4 * R))

@@ -17,9 +17,14 @@ ACT = mybir.ActivationFunctionType
 MULT = mybir.AluOpType.mult
 
 P = 128
+PASS = 512
 PASSES = 2 * G
 TILES = 4 * G
+PIECES = 4 * G
 HALF = 256
+RUN = 2
+
+X_PIECES_OF_STEP = ([6, 7], [8, 9, 10, 11], [12, 13], [14], [15], [], [])
 
 
 def tile_ping_pair_correlation_power_k7_kernel(
@@ -40,18 +45,17 @@ def tile_ping_pair_correlation_power_k7_kernel(
 
         vs_raw = keep.tile([P, PASSES * F], U8, name="vs_raw")
         nc.vector.memset(vs_raw[:, 0 : 2 * F].bitcast(I32), 0)
-        nc.vector.memset(vs_raw[:, 2 * F :].bitcast(I32), 0)
-        gain_raw = keep.tile([P, 512], BF16, name="gain_raw")
-        sorted_gain = keep.tile([P, 512], F32, name="sorted_gain")
-        nc.gpsimd.memset(sorted_gain[:], 0.0)
+        gain_raw = keep.tile([P, PASS], BF16, name="gain_raw")
+        sorted_gain = keep.tile([P, PASS], F32, name="sorted_gain")
+        nc.vector.memset(sorted_gain[:], 0.0)
 
         x_raw, v_raw, s_raw = {}, {}, {}
 
-        def load_x(m):
-            b, g, half = m // 4, m // 2 % 2, m % 2
-            x_raw[m] = keep.tile([P, 2, 512], BF16, name="x_raw%d" % m)
-            rows = x[b, HALF * half : HALF * (half + 1), 512 * g : 512 * (g + 1)]
-            nc.sync.dma_start(out=x_raw[m][:], in_=rows.rearrange("(j p) k -> p j k", j=2))
+        def load_x(piece):
+            b, g, half = piece // 4, piece // 2 % 2, piece % 2
+            x_raw[piece] = keep.tile([P, 2, PASS], BF16, name="x_raw%d" % piece)
+            rows = x[b, HALF * half : HALF * (half + 1), PASS * g : PASS * (g + 1)]
+            nc.sync.dma_start(out=x_raw[piece][:], in_=rows.rearrange("(j p) k -> p j k", j=2))
 
         def load_v_words(first, last):
             v_raw[first] = keep.tile([P, (last - first) * 2 * F], U8, name="v_raw%d" % first)
@@ -61,10 +65,11 @@ def tile_ping_pair_correlation_power_k7_kernel(
             )
 
         def load_v_scales(b):
-            for q in range(4):
+            for quad in range(4):
+                rows = vs_raw[32 * quad : 32 * quad + 4, 2 * F * b : 2 * F * (b + 1)]
                 nc.sync.dma_start(
-                    out=vs_raw[32 * q : 32 * q + 4, 2 * F * b : 2 * F * (b + 1)].bitcast(I32).rearrange("p (g w) -> p g w", g=2),
-                    in_=v_scales[2 * b : 2 * b + 2, 4 * q : 4 * q + 4, :].bitcast(I32).rearrange("g r w -> r g w"),
+                    out=rows.bitcast(I32).rearrange("p (g w) -> p g w", g=2),
+                    in_=v_scales[2 * b : 2 * b + 2, 4 * quad : 4 * quad + 4, :].bitcast(I32).rearrange("g r w -> r g w"),
                 )
 
         def load_second(a):
@@ -74,48 +79,24 @@ def tile_ping_pair_correlation_power_k7_kernel(
             for t in range(4):
                 nc.sync.dma_start(out=s_raw[a][:, t, :], in_=rows[h, t])
 
-        load_x(0)
-        load_x(1)
-        load_v_words(0, 1)
-        load_x(2)
-        load_x(3)
-        load_v_scales(0)
-        load_v_words(1, 2)
-        nc.sync.dma_start(out=gain_raw[0:8, :], in_=range_gain.rearrange("b (h f) -> (b h) f", h=2))
-        nc.sync.dma_start(out=gain_raw[32:48, 0:P], in_=row_gain.rearrange("b (j r) -> (b j) r", j=4))
-        nc.sync.dma_start(out=gain_raw[64:80, 0:P], in_=col_gain.rearrange("b (j d) -> (b j) d", j=4))
-        load_second(0)
-        load_x(4)
-        load_x(5)
-        load_second(1)
-        load_x(6)
-        load_x(7)
-        for b in range(1, G):
-            load_v_words(2 * b, 2 * b + 2)
-            load_v_scales(b)
-            for h in range(2):
-                for m in range(4 * b + 4 + 2 * h, min(4 * b + 6 + 2 * h, TILES)):
-                    load_x(m)
-                load_second(2 * b + h)
-
         def tr_bank():
-            return psum.tile([P, 512], F32, name="tr_bank", tag="tr", bufs=2)
+            return psum.tile([P, PASS], F32, name="tr_bank", tag="tr", bufs=2)
 
         def mm_bank():
-            return psum.tile([P, 512], F32, name="mm_bank", tag="mm", bufs=3)
+            return psum.tile([P, PASS], F32, name="mm_bank", tag="mm", bufs=3)
 
         gains = psum.tile([P, 4, P], F32, name="gains")
         rg_cols = keep.tile([P, TILES], F32, name="rg_cols")
         cg_cols = keep.tile([P, TILES], F32, name="cg_cols")
-        cg = {}
+        cg_spread = {}
 
         def sort_gains():
-            nc.vector.tensor_copy(
+            nc.scalar.copy(
                 out=sorted_gain[0:8, :].rearrange("p (t q r) -> p t q r", t=4, r=8),
                 in_=gain_raw[0:8, :].rearrange("p (q t r) -> p t q r", t=4, r=8),
             )
-            nc.vector.tensor_copy(out=sorted_gain[32:48, 0:P], in_=gain_raw[32:48, 0:P])
-            nc.vector.tensor_copy(out=sorted_gain[64:80, 0:P], in_=gain_raw[64:80, 0:P])
+            nc.scalar.copy(out=sorted_gain[32:48, 0:P], in_=gain_raw[32:48, 0:P])
+            nc.scalar.copy(out=sorted_gain[64:80, 0:P], in_=gain_raw[64:80, 0:P])
 
         def transpose_gains():
             for t in range(4):
@@ -124,48 +105,48 @@ def tile_ping_pair_correlation_power_k7_kernel(
             nc.scalar.copy(out=cg_cols[:], in_=gains[:, 0, 64:80])
 
         def spread_col_gain(b):
-            cg[b] = psum.tile([P, N], F32, name="cg", bufs=2)
+            cg_spread[b] = psum.tile([P, N], F32, name="cg", bufs=2)
             for j in range(4):
                 column = cg_cols[:, 4 * b + j : 4 * b + j + 1]
-                nc.tensor.transpose(cg[b][:, P * j : P * (j + 1)], column.to_broadcast([P, P]), ident[:])
+                nc.tensor.transpose(cg_spread[b][:, P * j : P * (j + 1)], column.to_broadcast([P, P]), ident[:])
 
-        in_order, x_t, x_codes, x_scales = {}, {}, {}, {}
+        x_sorted, x_t, x_codes, x_scales = {}, {}, {}, {}
         v_sorted, vs_sorted = {}, {}
         e_bank, tanh_e, h_bf, h_codes, h_scales = {}, {}, {}, {}, {}
-        s_il, s_codes, s_scales = {}, {}, {}
-        c_bank, sq, y, y_bf, y_t = {}, {}, {}, {}, {}
+        s_slots, s_codes, s_scales = {}, {}, {}
+        sq, y, y_bf, y_t = {}, {}, {}, {}
         y_scales = keep.tile([P, G * R], U8, name="y_scales", align_bytes=64)
 
-        def sort_x(m):
-            in_order[m] = work.tile([P, 512], F32, name="in_order")
+        def sort_x(piece):
+            x_sorted[piece] = work.tile([P, PASS], F32, name="in_order")
             nc.vector.tensor_copy(
-                out=in_order[m][:].rearrange("p (j u k) -> p j u k", j=2, u=2),
-                in_=x_raw[m][:].bitcast(F32).rearrange("p j (k u) -> p j u k", u=2),
+                out=x_sorted[piece][:].rearrange("p (j u k) -> p j u k", j=2, u=2),
+                in_=x_raw[piece][:].bitcast(F32).rearrange("p j (k u) -> p j u k", u=2),
             )
 
-        def turn_x(m):
-            i, half = divmod(m, 2)
-            words = x_raw[m][:].bitcast(F32)
+        def turn_x(piece):
+            x_pass, half = divmod(piece, 2)
+            words = x_raw[piece][:].bitcast(F32)
             bank = tr_bank()
             for j in range(2):
                 for u in range(2):
                     c = P * (2 * j + u)
-                    src = in_order[m][:, c : c + P] if m in in_order else words[:, j, u:256:2]
+                    src = x_sorted[piece][:, c : c + P] if piece in x_sorted else words[:, j, u : 2 * P : 2]
                     nc.tensor.transpose(bank[:, c : c + P], src, ident[:])
             if half == 0:
-                x_t[i] = work.tile([P, R * 4], BF16, name="x_t", bufs=3, align_bytes=64)
-            dst = x_t[i][:, 4 * HALF * half : 4 * HALF * (half + 1)].bitcast(F32)
+                x_t[x_pass] = work.tile([P, R * 4], BF16, name="x_t", bufs=3, align_bytes=64)
+            dst = x_t[x_pass][:, 4 * HALF * half : 4 * HALF * (half + 1)].bitcast(F32)
             nc.scalar.copy(
                 out=dst.rearrange("p (j r u) -> p j r u", j=2, u=2), in_=bank[:].rearrange("p (j u r) -> p j r u", j=2, u=2)
             )
 
-        def quantize_x(i):
-            b, g = divmod(i, 2)
+        def quantize_x(x_pass):
+            b, g = divmod(x_pass, 2)
             if g == 0:
                 x_codes[b] = work.tile([P, 2 * R], U32, name="x_codes", align_bytes=64)
                 x_scales[b] = work.tile([P, 2 * R], U8, name="x_scales", align_bytes=64)
             cols = slice(R * g, R * (g + 1))
-            nc.vector.quantize_mx(out=x_codes[b][:, cols].bitcast(FP8X4), scales=x_scales[b][:, cols], in_=x_t[i][:])
+            nc.vector.quantize_mx(out=x_codes[b][:, cols].bitcast(FP8X4), scales=x_scales[b][:, cols], in_=x_t[x_pass][:])
 
         def sort_v(first, last):
             b, g = divmod(first, 2)
@@ -178,17 +159,17 @@ def tile_ping_pair_correlation_power_k7_kernel(
                 (vs_sorted[b][:, F * g : F * (g + count)], vs_raw[:, F * first : F * last]),
             ):
                 nc.vector.tensor_copy(
-                    out=dst.bitcast(I32).rearrange("p (a t q w) -> p a t q w", a=2 * count, t=4, q=16),
-                    in_=src.bitcast(I32).rearrange("p (a q t w) -> p a t q w", a=2 * count, t=4, q=16),
+                    out=dst.bitcast(I32).rearrange("p (gh t q w) -> p gh t q w", gh=2 * count, t=4, q=16),
+                    in_=src.bitcast(I32).rearrange("p (gh q t w) -> p gh t q w", gh=2 * count, t=4, q=16),
                 )
 
-        def filter_pass(k, g):
-            b, s = divmod(k, 8)
+        def filter_pass(e, g):
+            b, ht = divmod(e, 8)
             if g == 0:
-                e_bank[k] = mm_bank()
-            c = P * (8 * g + s)
+                e_bank[e] = mm_bank()
+            c = P * (8 * g + ht)
             nc.tensor.matmul_mx(
-                out=e_bank[k][:],
+                out=e_bank[e][:],
                 lhsT=v_sorted[b][:, 2 * c : 2 * (c + P)].bitcast(FP4X4),
                 lhsT_scale=vs_sorted[b][:, c : c + P],
                 rhs=x_codes[b][:, R * g : R * (g + 1)].bitcast(FP8X4),
@@ -197,24 +178,24 @@ def tile_ping_pair_correlation_power_k7_kernel(
                 stop=(g == 1),
             )
 
-        def limit(k):
-            a, t = divmod(k, 4)
+        def limit(e):
+            a, t = divmod(e, 4)
             if t == 0:
                 tanh_e[a] = work.tile([P, 4, R], F32, name="tanh_e", bufs=3)
-            nc.scalar.activation(out=tanh_e[a][:, t, :], in_=e_bank[k][:], func=ACT.Tanh)
+            nc.scalar.activation(out=tanh_e[a][:, t, :], in_=e_bank[e][:], func=ACT.Tanh)
 
-        def filter_and_limit(k):
-            filter_pass(k, 0)
-            filter_pass(k, 1)
-            limit(k)
+        def filter_and_limit(e):
+            filter_pass(e, 0)
+            filter_pass(e, 1)
+            limit(e)
 
         def apply_range_gain(a, first, last):
             if first == 0:
                 h_bf[a] = work.tile([P, R * 4], BF16, name="h_bf", align_bytes=64)
             nc.vector.tensor_tensor(
-                out=h_bf[a][:, 4 * first : 4 * last].rearrange("p (c i t) -> p c t i", i=2, t=4),
-                in0=tanh_e[a][:, :, first:last].rearrange("p t (c i) -> p c t i", i=2),
-                in1=gains[:, :, a : a + 1].unsqueeze(1).to_broadcast([P, (last - first) // 2, 4, 2]),
+                out=h_bf[a][:, 4 * first : 4 * last].rearrange("p (c i t) -> p c t i", i=RUN, t=4),
+                in0=tanh_e[a][:, :, first:last].rearrange("p t (c i) -> p c t i", i=RUN),
+                in1=gains[:, :, a : a + 1].unsqueeze(1).to_broadcast([P, (last - first) // RUN, 4, RUN]),
                 op=MULT,
             )
 
@@ -228,25 +209,22 @@ def tile_ping_pair_correlation_power_k7_kernel(
                 out=h_codes[b][:, cols].bitcast(FP8X4), scales=h_scales[b][:, cols], in_=h_bf[a][:, 4 * first : 4 * last]
             )
 
-        def second_piece(a, first, last, name, bufs):
-            piece = work.tile([P, 4 * (last - first)], BF16, name=name, bufs=bufs, align_bytes=64)
-            s_il[a, first] = piece
-            return piece[:], s_raw[a][:, :, first:last]
+        def second_columns(a, first, last, name):
+            s_slots[a, first] = work.tile([P, 4 * (last - first)], BF16, name=name, bufs=1, align_bytes=64)
+            return s_slots[a, first][:], s_raw[a][:, :, first:last]
+
+        def copy_on_gpsimd(dst, src):
+            nc.gpsimd.tensor_scalar(out=dst, in0=src, scalar1=1.0, scalar2=1.0, op0=MULT, op1=MULT)
 
         def interleave_on_gpsimd(a, first, last):
-            dst, src = second_piece(a, first, last, "s_il_gpsimd", 1)
-            nc.gpsimd.tensor_scalar(
-                out=dst.rearrange("p (c t) -> p c t", t=4),
-                in0=src.rearrange("p t c -> p c t"),
-                scalar1=1.0,
-                scalar2=1.0,
-                op0=MULT,
-                op1=MULT,
-            )
+            dst, src = second_columns(a, first, last, "s_il_gpsimd")
+            copy_on_gpsimd(dst.rearrange("p (c t) -> p c t", t=4), src.rearrange("p t c -> p c t"))
 
-        def interleave_by_copy(a, first, last, copy):
-            dst, src = second_piece(a, first, last, "s_il", 3)
-            copy(out=dst.rearrange("p (c i t) -> p c t i", i=4, t=4), in_=src.rearrange("p t (c i) -> p c t i", i=4))
+        def interleave_on_vector(a, first, last, name):
+            dst, src = second_columns(a, first, last, name)
+            nc.vector.tensor_copy(
+                out=dst.rearrange("p (c i t) -> p c t i", i=4, t=4), in_=src.rearrange("p t (c i) -> p c t i", i=4)
+            )
 
         def quantize_second(a, first, last):
             b, h = divmod(a, 2)
@@ -254,7 +232,9 @@ def tile_ping_pair_correlation_power_k7_kernel(
                 s_codes[b] = work.tile([P, 2 * N], U32, name="s_codes", align_bytes=64)
                 s_scales[b] = work.tile([P, 2 * N], U8, name="s_scales", align_bytes=64)
             cols = slice(N * h + first, N * h + last)
-            nc.vector.quantize_mx(out=s_codes[b][:, cols].bitcast(FP8X4), scales=s_scales[b][:, cols], in_=s_il[a, first][:])
+            nc.vector.quantize_mx(
+                out=s_codes[b][:, cols].bitcast(FP8X4), scales=s_scales[b][:, cols], in_=s_slots[a, first][:]
+            )
 
         def correlate_and_square(m):
             b, j = divmod(m, 4)
@@ -281,7 +261,7 @@ def tile_ping_pair_correlation_power_k7_kernel(
                 out=y[pair][:, N * j : N * (j + 1)],
                 in0=sq[m][:],
                 scalar=rg_cols[:, m : m + 1],
-                in1=cg[m // 4][:],
+                in1=cg_spread[m // 4][:],
                 op0=MULT,
                 op1=MULT,
             )
@@ -295,39 +275,32 @@ def tile_ping_pair_correlation_power_k7_kernel(
                 in_=y[pair][:, N * j : N * (j + count)].rearrange("p (j d) -> p j d", d=N),
             )
 
-        def round_y(first, last, copy):
+        def rounding_operands(first, last):
             pair, j = divmod(first, 2)
-            if j == 0:
+            if pair not in y_bf:
                 y_bf[pair] = work.tile([P, 2 * N], BF16, name="y_bf", bufs=3)
             cols = slice(N * j, N * (j + last - first))
+            return y_bf[pair][:, cols], y[pair][:, cols]
+
+        def round_y(first, last, copy):
+            dst, src = rounding_operands(first, last)
             copy(
-                out=y_bf[pair][:, cols].rearrange("p (j u k e) -> p j u k e", u=2, k=P, e=2),
-                in_=y[pair][:, cols].rearrange("p (j k u e) -> p j u k e", u=2, k=P, e=2),
+                out=dst.rearrange("p (j u k e) -> p j u k e", u=2, k=P, e=2),
+                in_=src.rearrange("p (j k u e) -> p j u k e", u=2, k=P, e=2),
             )
 
         def round_y_on_gpsimd(m):
-            pair, j = divmod(m, 2)
-            if j == 0:
-                y_bf[pair] = work.tile([P, 2 * N], BF16, name="y_bf", bufs=3)
-            cols = slice(N * j, N * (j + 1))
-            nc.gpsimd.tensor_scalar(
-                out=y_bf[pair][:, cols].rearrange("p (u k e) -> p u k e", u=2, e=2),
-                in0=y[pair][:, cols].rearrange("p (k u e) -> p u k e", u=2, e=2),
-                scalar1=1.0,
-                scalar2=1.0,
-                op0=MULT,
-                op1=MULT,
-            )
+            dst, src = rounding_operands(m, m + 1)
+            copy_on_gpsimd(dst.rearrange("p (u k e) -> p u k e", u=2, e=2), src.rearrange("p (k u e) -> p u k e", u=2, e=2))
 
-        def turn_y(first, last, copy):
+        def turn_y(first, last, copy, bank):
             pair, j = divmod(first, 2)
             count = last - first
             words = y_bf[pair][:].bitcast(F32)
-            bank = tr_bank()
             for c in range(0, 2 * P * count, P):
                 nc.tensor.transpose(bank[:, c : c + P], words[:, 2 * P * j + c : 2 * P * j + c + P], ident[:])
             if j == 0:
-                y_t[pair] = work.tile([P, HALF * 4], BF16, name="y_t", align_bytes=64)
+                y_t[pair] = work.tile([P, HALF * 4], BF16, name="y_t", bufs=3, align_bytes=64)
             dst = y_t[pair][:, 4 * P * j : 4 * P * (j + count)].bitcast(F32)
             copy(
                 out=dst.rearrange("p (j r u) -> p j r u", r=P, u=2),
@@ -343,54 +316,83 @@ def tile_ping_pair_correlation_power_k7_kernel(
             )
 
         def store_scales(cols):
-            for q in range(4):
+            for quad in range(4):
                 nc.sync.dma_start(
-                    out=out_2[0, 4 * q : 4 * q + 4, cols].bitcast(I32), in_=y_scales[32 * q : 32 * q + 4, cols].bitcast(I32)
+                    out=out_2[0, 4 * quad : 4 * quad + 4, cols].bitcast(I32),
+                    in_=y_scales[32 * quad : 32 * quad + 4, cols].bitcast(I32),
                 )
 
-        for m in range(4):
-            sort_x(m)
-            turn_x(m)
+        load_x(0)
+        load_x(1)
+        load_v_words(0, 1)
+        load_x(2)
+        load_x(3)
+        load_v_scales(0)
+        load_v_words(1, 2)
+        nc.gpsimd.dma_start(out=gain_raw[0:8, :], in_=range_gain.rearrange("b (h f) -> (b h) f", h=2))
+        nc.gpsimd.dma_start(out=gain_raw[32:48, 0:P], in_=row_gain.rearrange("b (j r) -> (b j) r", j=4))
+        nc.gpsimd.dma_start(out=gain_raw[64:80, 0:P], in_=col_gain.rearrange("b (j d) -> (b j) d", j=4))
+        load_second(0)
+        load_x(4)
+        load_x(5)
+        load_second(1)
+        for piece in range(2):
+            sort_x(piece)
+            turn_x(piece)
+        nc.vector.memset(vs_raw[:, 2 * F :].bitcast(I32), 0)
+        load_x(6)
+        load_x(7)
+        for b in range(1, G):
+            load_v_words(2 * b, 2 * b + 2)
+            load_v_scales(b)
+            for h in range(2):
+                for piece in range(4 * b + 4 + 2 * h, min(4 * b + 6 + 2 * h, PIECES)):
+                    load_x(piece)
+                load_second(2 * b + h)
+
+        for piece in range(2, 4):
+            sort_x(piece)
+            turn_x(piece)
+        sort_gains()
         quantize_x(0)
         sort_v(0, 1)
         sort_v(1, 2)
         quantize_x(1)
         for g in range(2):
-            for k in range(3):
-                filter_pass(k, g)
-        for k in range(3):
-            limit(k)
+            for e in range(2):
+                filter_pass(e, g)
+        for e in range(2):
+            limit(e)
+        filter_and_limit(2)
         filter_and_limit(3)
-        sort_gains()
         transpose_gains()
         turn_x(4)
         turn_x(5)
-        interleave_by_copy(0, 0, HALF, nc.vector.tensor_copy)
-        interleave_by_copy(0, HALF, N, nc.vector.tensor_copy)
+        interleave_on_vector(0, 0, HALF, "s_il")
+        interleave_on_vector(0, HALF, N, "s_il_gpsimd")
         quantize_second(0, 0, HALF)
         quantize_second(0, HALF, N)
 
         for a in range(PASSES - 1):
-            gpsimd_first = HALF if a < 2 else 0
+            gpsimd_first = HALF if a == 1 else 0
+            x_pieces = X_PIECES_OF_STEP[a]
+            early = 2 if a < 2 else 1
+
             if a >= 2:
                 correlate_and_square(2 * a - 4)
                 correlate_and_square(2 * a - 3)
-            x_units = ([6, 7], [8, 9, 10, 11])[a] if a < 2 else [m for m in (2 * a + 8, 2 * a + 9) if m < TILES]
-            early = 2 if a < 2 else 1
             filter_and_limit(4 * a + 4)
             filter_and_limit(4 * a + 5)
-            for m in x_units[:early]:
-                turn_x(m)
+            for piece in x_pieces[:early]:
+                turn_x(piece)
             if a % 2 == 1:
                 spread_col_gain(a // 2)
             filter_and_limit(4 * a + 6)
             filter_and_limit(4 * a + 7)
-            for m in x_units[early:]:
-                turn_x(m)
-            if a == 0:
-                interleave_by_copy(1, 0, HALF, nc.scalar.copy)
+            for piece in x_pieces[early:]:
+                turn_x(piece)
             if a >= 3:
-                turn_y(2 * a - 6, 2 * a - 4, nc.scalar.copy)
+                turn_y(2 * a - 6, 2 * a - 4, nc.scalar.copy, tr_bank())
 
             interleave_on_gpsimd(a + 1, gpsimd_first, N)
             apply_range_gain(a, 0, R)
@@ -399,14 +401,14 @@ def tile_ping_pair_correlation_power_k7_kernel(
                 weigh(2 * a - 3)
                 store_y(2 * a - 4, 2 * a - 2)
                 round_y(2 * a - 4, 2 * a - 2, nc.scalar.copy)
+
             if a == 0:
                 quantize_x(2)
             if a == 1:
-                interleave_by_copy(2, 0, HALF, nc.vector.tensor_copy)
-                quantize_second(1, 0, HALF)
+                interleave_on_vector(2, 0, HALF, "s_il")
             if a % 2 == 0 and a + 2 < PASSES:
                 sort_v(a + 2, a + 4)
-            if a + 3 < PASSES and a != 1:
+            if a != 1 and a + 3 < PASSES:
                 quantize_x(a + 3)
             quantize_h(a, 0, R)
             if a == 1:
@@ -416,34 +418,42 @@ def tile_ping_pair_correlation_power_k7_kernel(
                 quantize_y(a - 4)
             quantize_second(a + 1, gpsimd_first, N)
 
+        last_pass = PASSES - 1
         spread_col_gain(G - 1)
         correlate_and_square(10)
         correlate_and_square(11)
-        turn_y(8, 10, nc.scalar.copy)
-        apply_range_gain(7, 0, HALF)
+        turn_y(8, 10, nc.scalar.copy, tr_bank())
+        apply_range_gain(last_pass, 0, HALF)
         quantize_y(3)
         store_scales(slice(0, 2 * R))
-        quantize_h(7, 0, HALF)
+        quantize_h(last_pass, 0, HALF)
         correlate_and_square(12)
         correlate_and_square(13)
-        apply_range_gain(7, HALF, R)
-        quantize_y(4)
-        quantize_h(7, HALF, R)
+        apply_range_gain(last_pass, HALF, R)
         weigh(10)
+        quantize_h(last_pass, HALF, R)
+        quantize_y(4)
         correlate_and_square(14)
         correlate_and_square(15)
-        for m in range(11, TILES):
-            weigh(m)
-            if m % 2 == 1 or m == TILES - 2:
-                store_y(m - 1 if m < TILES - 2 else m, m + 1)
-            if m - 1 < TILES - 2:
-                round_y_on_gpsimd(m - 1)
-        turn_y(10, 12, nc.scalar.copy)
-        round_y(14, 15, nc.scalar.copy)
-        quantize_y(5)
+        weigh(11)
+        store_y(10, 12)
+        round_y_on_gpsimd(11)
+        round_y(10, 11, nc.scalar.copy)
+        weigh(12)
+        weigh(13)
+        store_y(12, 14)
+        round_y(12, 13, nc.scalar.copy)
+        round_y_on_gpsimd(13)
+        turn_y(10, 12, nc.scalar.copy, tr_bank())
+        weigh(14)
+        store_y(14, 15)
+        weigh(15)
+        store_y(15, 16)
+        round_y(14, 15, nc.vector.tensor_copy)
         round_y(15, 16, nc.vector.tensor_copy)
-        turn_y(12, 14, nc.vector.tensor_copy)
-        turn_y(14, 16, nc.scalar.copy)
-        quantize_y(6)
-        quantize_y(7)
+        turn_y(12, 14, nc.vector.tensor_copy, tr_bank())
+        turn_y(14, 15, nc.scalar.copy, mm_bank())
+        turn_y(15, 16, nc.scalar.copy, mm_bank())
+        for pair in range(5, 8):
+            quantize_y(pair)
         store_scales(slice(2 * R, 4 * R))

from contextlib import ExitStack

import concourse.mybir as mybir
from concourse.masks import make_identity

G, R, K, F, N = 4, 512, 1024, 1024, 512
FLOPS = 2 * G * R * K * F + 2 * G * R * F * N

F32 = mybir.dt.float32
BF16 = mybir.dt.bfloat16
I32 = mybir.dt.int32
U32 = mybir.dt.uint32
U8 = mybir.dt.uint8
FP8X4 = mybir.dt.float8_e4m3fn_x4
FP4X4 = mybir.dt.float4_e2m1fn_x4
ACT = mybir.ActivationFunctionType
MULT = mybir.AluOpType.mult

P = 128
PASS = 512
PASSES = 2 * G
TILES = 4 * G
PIECES = 4 * G
HALF = 256
RUN = 2

X_PIECES_OF_STEP = ([6, 7], [8, 9, 10, 11], [12, 13], [14], [15], [], [])


def tile_ping_pair_correlation_power_k7_kernel(
    tc, x, v_words, v_scales, range_gain, second, row_gain, col_gain, out_0, out_1, out_2
):
    nc = tc.nc
    with ExitStack() as ctx:
        keep = ctx.enter_context(tc.tile_pool(name="keep", bufs=1))
        work = ctx.enter_context(tc.tile_pool(name="work", bufs=2))
        psum = ctx.enter_context(tc.psum_pool(name="psum", bufs=1))
        ctx.enter_context(tc.manual_schedule())

        ident = keep.tile([P, P], F32, name="ident")
        make_identity(nc, ident[:])
        warm = keep.tile([P, 8], F32, name="warm")
        nc.vector.memset(warm[:], 0.0)
        nc.scalar.activation(out=warm[:, 4:5], in_=warm[:, 0:1], func=ACT.Tanh)

        vs_raw = keep.tile([P, PASSES * F], U8, name="vs_raw")
        nc.vector.memset(vs_raw[:, 0 : 2 * F].bitcast(I32), 0)
        gain_raw = keep.tile([P, PASS], BF16, name="gain_raw")
        sorted_gain = keep.tile([P, PASS], F32, name="sorted_gain")
        nc.vector.memset(sorted_gain[:], 0.0)

        x_raw, v_raw, s_raw = {}, {}, {}

        def load_x(piece):
            b, g, half = piece // 4, piece // 2 % 2, piece % 2
            x_raw[piece] = keep.tile([P, 2, PASS], BF16, name="x_raw%d" % piece)
            rows = x[b, HALF * half : HALF * (half + 1), PASS * g : PASS * (g + 1)]
            nc.sync.dma_start(out=x_raw[piece][:], in_=rows.rearrange("(j p) k -> p j k", j=2))

        def load_v_words(first, last):
            v_raw[first] = keep.tile([P, (last - first) * 2 * F], U8, name="v_raw%d" % first)
            nc.sync.dma_start(
                out=v_raw[first][:].bitcast(I32).rearrange("p (g w) -> p g w", g=last - first),
                in_=v_words[first:last].bitcast(I32).rearrange("g p w -> p g w"),
            )

        def load_v_scales(b):
            for quad in range(4):
                rows = vs_raw[32 * quad : 32 * quad + 4, 2 * F * b : 2 * F * (b + 1)]
                nc.sync.dma_start(
                    out=rows.bitcast(I32).rearrange("p (g w) -> p g w", g=2),
                    in_=v_scales[2 * b : 2 * b + 2, 4 * quad : 4 * quad + 4, :].bitcast(I32).rearrange("g r w -> r g w"),
                )

        def load_second(a):
            b, h = divmod(a, 2)
            rows = second[b].rearrange("(h q t r) d -> h t q r d", h=2, t=4, r=8)
            s_raw[a] = keep.tile([P, 4, N], BF16, name="s_raw%d" % a)
            for t in range(4):
                nc.sync.dma_start(out=s_raw[a][:, t, :], in_=rows[h, t])

        def tr_bank():
            return psum.tile([P, PASS], F32, name="tr_bank", tag="tr", bufs=2)

        def mm_bank():
            return psum.tile([P, PASS], F32, name="mm_bank", tag="mm", bufs=3)

        gains = psum.tile([P, 4, P], F32, name="gains")
        rg_cols = keep.tile([P, TILES], F32, name="rg_cols")
        cg_cols = keep.tile([P, TILES], F32, name="cg_cols")
        cg_spread = {}

        def sort_gains():
            nc.scalar.copy(
                out=sorted_gain[0:8, :].rearrange("p (t q r) -> p t q r", t=4, r=8),
                in_=gain_raw[0:8, :].rearrange("p (q t r) -> p t q r", t=4, r=8),
            )
            nc.scalar.copy(out=sorted_gain[32:48, 0:P], in_=gain_raw[32:48, 0:P])
            nc.scalar.copy(out=sorted_gain[64:80, 0:P], in_=gain_raw[64:80, 0:P])

        def transpose_gains():
            for t in range(4):
                nc.tensor.transpose(gains[:, t, :], sorted_gain[:, P * t : P * (t + 1)], ident[:])
            nc.scalar.copy(out=rg_cols[:], in_=gains[:, 0, 32:48])
            nc.scalar.copy(out=cg_cols[:], in_=gains[:, 0, 64:80])

        def spread_col_gain(b):
            cg_spread[b] = psum.tile([P, N], F32, name="cg", bufs=2)
            for j in range(4):
                column = cg_cols[:, 4 * b + j : 4 * b + j + 1]
                nc.tensor.transpose(cg_spread[b][:, P * j : P * (j + 1)], column.to_broadcast([P, P]), ident[:])

        x_sorted, x_t, x_codes, x_scales = {}, {}, {}, {}
        v_sorted, vs_sorted = {}, {}
        e_bank, tanh_e, h_bf, h_codes, h_scales = {}, {}, {}, {}, {}
        s_slots, s_codes, s_scales = {}, {}, {}
        sq, y, y_bf, y_t = {}, {}, {}, {}
        y_scales = keep.tile([P, G * R], U8, name="y_scales", align_bytes=64)

        def sort_x(piece):
            x_sorted[piece] = work.tile([P, PASS], F32, name="in_order")
            nc.vector.tensor_copy(
                out=x_sorted[piece][:].rearrange("p (j u k) -> p j u k", j=2, u=2),
                in_=x_raw[piece][:].bitcast(F32).rearrange("p j (k u) -> p j u k", u=2),
            )

        def turn_x(piece):
            x_pass, half = divmod(piece, 2)
            words = x_raw[piece][:].bitcast(F32)
            bank = tr_bank()
            for j in range(2):
                for u in range(2):
                    c = P * (2 * j + u)
                    src = x_sorted[piece][:, c : c + P] if piece in x_sorted else words[:, j, u : 2 * P : 2]
                    nc.tensor.transpose(bank[:, c : c + P], src, ident[:])
            if half == 0:
                x_t[x_pass] = work.tile([P, R * 4], BF16, name="x_t", bufs=3, align_bytes=64)
            dst = x_t[x_pass][:, 4 * HALF * half : 4 * HALF * (half + 1)].bitcast(F32)
            nc.scalar.copy(
                out=dst.rearrange("p (j r u) -> p j r u", j=2, u=2), in_=bank[:].rearrange("p (j u r) -> p j r u", j=2, u=2)
            )

        def quantize_x(x_pass):
            b, g = divmod(x_pass, 2)
            if g == 0:
                x_codes[b] = work.tile([P, 2 * R], U32, name="x_codes", align_bytes=64)
                x_scales[b] = work.tile([P, 2 * R], U8, name="x_scales", align_bytes=64)
            cols = slice(R * g, R * (g + 1))
            nc.vector.quantize_mx(out=x_codes[b][:, cols].bitcast(FP8X4), scales=x_scales[b][:, cols], in_=x_t[x_pass][:])

        def sort_v(first, last):
            b, g = divmod(first, 2)
            if g == 0:
                v_sorted[b] = work.tile([P, 4 * F], U8, name="v_sorted", align_bytes=64)
                vs_sorted[b] = work.tile([P, 2 * F], U8, name="vs_sorted", align_bytes=64)
            count = last - first
            for dst, src in (
                (v_sorted[b][:, 2 * F * g : 2 * F * (g + count)], v_raw[first][:]),
                (vs_sorted[b][:, F * g : F * (g + count)], vs_raw[:, F * first : F * last]),
            ):
                nc.vector.tensor_copy(
                    out=dst.bitcast(I32).rearrange("p (gh t q w) -> p gh t q w", gh=2 * count, t=4, q=16),
                    in_=src.bitcast(I32).rearrange("p (gh q t w) -> p gh t q w", gh=2 * count, t=4, q=16),
                )

        def filter_pass(e, g):
            b, ht = divmod(e, 8)
            if g == 0:
                e_bank[e] = mm_bank()
            c = P * (8 * g + ht)
            nc.tensor.matmul_mx(
                out=e_bank[e][:],
                lhsT=v_sorted[b][:, 2 * c : 2 * (c + P)].bitcast(FP4X4),
                lhsT_scale=vs_sorted[b][:, c : c + P],
                rhs=x_codes[b][:, R * g : R * (g + 1)].bitcast(FP8X4),
                rhs_scale=x_scales[b][:, R * g : R * (g + 1)],
                start=(g == 0),
                stop=(g == 1),
            )

        def limit(e):
            a, t = divmod(e, 4)
            if t == 0:
                tanh_e[a] = work.tile([P, 4, R], F32, name="tanh_e", bufs=3)
            nc.scalar.activation(out=tanh_e[a][:, t, :], in_=e_bank[e][:], func=ACT.Tanh)

        def filter_and_limit(e):
            filter_pass(e, 0)
            filter_pass(e, 1)
            limit(e)

        def apply_range_gain(a, first, last):
            if first == 0:
                h_bf[a] = work.tile([P, R * 4], BF16, name="h_bf", align_bytes=64)
            nc.vector.tensor_tensor(
                out=h_bf[a][:, 4 * first : 4 * last].rearrange("p (c i t) -> p c t i", i=RUN, t=4),
                in0=tanh_e[a][:, :, first:last].rearrange("p t (c i) -> p c t i", i=RUN),
                in1=gains[:, :, a : a + 1].unsqueeze(1).to_broadcast([P, (last - first) // RUN, 4, RUN]),
                op=MULT,
            )

        def quantize_h(a, first, last):
            b, h = divmod(a, 2)
            if h == 0:
                h_codes[b] = work.tile([P, 2 * R], U32, name="h_codes", align_bytes=64)
                h_scales[b] = work.tile([P, 2 * R], U8, name="h_scales", align_bytes=64)
            cols = slice(R * h + first, R * h + last)
            nc.vector.quantize_mx(
                out=h_codes[b][:, cols].bitcast(FP8X4), scales=h_scales[b][:, cols], in_=h_bf[a][:, 4 * first : 4 * last]
            )

        def second_columns(a, first, last, name):
            s_slots[a, first] = work.tile([P, 4 * (last - first)], BF16, name=name, bufs=1, align_bytes=64)
            return s_slots[a, first][:], s_raw[a][:, :, first:last]

        def copy_on_gpsimd(dst, src):
            nc.gpsimd.tensor_scalar(out=dst, in0=src, scalar1=1.0, scalar2=1.0, op0=MULT, op1=MULT)

        def interleave_on_gpsimd(a, first, last):
            dst, src = second_columns(a, first, last, "s_il_gpsimd")
            copy_on_gpsimd(dst.rearrange("p (c t) -> p c t", t=4), src.rearrange("p t c -> p c t"))

        def interleave_on_vector(a, first, last, name):
            dst, src = second_columns(a, first, last, name)
            nc.vector.tensor_copy(
                out=dst.rearrange("p (c i t) -> p c t i", i=4, t=4), in_=src.rearrange("p t (c i) -> p c t i", i=4)
            )

        def quantize_second(a, first, last):
            b, h = divmod(a, 2)
            if b not in s_codes:
                s_codes[b] = work.tile([P, 2 * N], U32, name="s_codes", align_bytes=64)
                s_scales[b] = work.tile([P, 2 * N], U8, name="s_scales", align_bytes=64)
            cols = slice(N * h + first, N * h + last)
            nc.vector.quantize_mx(
                out=s_codes[b][:, cols].bitcast(FP8X4), scales=s_scales[b][:, cols], in_=s_slots[a, first][:]
            )

        def correlate_and_square(m):
            b, j = divmod(m, 4)
            bank = mm_bank()
            for h in range(2):
                c = R * h + P * j
                nc.tensor.matmul_mx(
                    out=bank[:],
                    lhsT=h_codes[b][:, c : c + P].bitcast(FP8X4),
                    lhsT_scale=h_scales[b][:, c : c + P],
                    rhs=s_codes[b][:, N * h : N * (h + 1)].bitcast(FP8X4),
                    rhs_scale=s_scales[b][:, N * h : N * (h + 1)],
                    start=(h == 0),
                    stop=(h == 1),
                )
            sq[m] = work.tile([P, N], F32, name="sq", bufs=5)
            nc.scalar.activation(out=sq[m][:], in_=bank[:], func=ACT.Square)

        def weigh(m):
            pair, j = divmod(m, 2)
            if j == 0:
                y[pair] = work.tile([P, 2 * N], F32, name="y", bufs=3)
            nc.vector.scalar_tensor_tensor(
                out=y[pair][:, N * j : N * (j + 1)],
                in0=sq[m][:],
                scalar=rg_cols[:, m : m + 1],
                in1=cg_spread[m // 4][:],
                op0=MULT,
                op1=MULT,
            )

        def store_y(first, last):
            pair, j = divmod(first, 2)
            b, r0 = divmod(P * first, R)
            count = last - first
            nc.sync.dma_start(
                out=out_0[b, r0 : r0 + P * count, :].rearrange("(j p) d -> p j d", p=P),
                in_=y[pair][:, N * j : N * (j + count)].rearrange("p (j d) -> p j d", d=N),
            )

        def rounding_operands(first, last):
            pair, j = divmod(first, 2)
            if pair not in y_bf:
                y_bf[pair] = work.tile([P, 2 * N], BF16, name="y_bf", bufs=3)
            cols = slice(N * j, N * (j + last - first))
            return y_bf[pair][:, cols], y[pair][:, cols]

        def round_y(first, last, copy):
            dst, src = rounding_operands(first, last)
            copy(
                out=dst.rearrange("p (j u k e) -> p j u k e", u=2, k=P, e=2),
                in_=src.rearrange("p (j k u e) -> p j u k e", u=2, k=P, e=2),
            )

        def round_y_on_gpsimd(m):
            dst, src = rounding_operands(m, m + 1)
            copy_on_gpsimd(dst.rearrange("p (u k e) -> p u k e", u=2, e=2), src.rearrange("p (k u e) -> p u k e", u=2, e=2))

        def turn_y(first, last, copy, bank):
            pair, j = divmod(first, 2)
            count = last - first
            words = y_bf[pair][:].bitcast(F32)
            for c in range(0, 2 * P * count, P):
                nc.tensor.transpose(bank[:, c : c + P], words[:, 2 * P * j + c : 2 * P * j + c + P], ident[:])
            if j == 0:
                y_t[pair] = work.tile([P, HALF * 4], BF16, name="y_t", bufs=3, align_bytes=64)
            dst = y_t[pair][:, 4 * P * j : 4 * P * (j + count)].bitcast(F32)
            copy(
                out=dst.rearrange("p (j r u) -> p j r u", r=P, u=2),
                in_=bank[:, 0 : 2 * P * count].rearrange("p (j u r) -> p j r u", r=P, u=2),
            )

        def quantize_y(pair):
            cols = slice(HALF * pair, HALF * (pair + 1))
            y_codes = work.tile([P, HALF], U32, name="y_codes", bufs=4, align_bytes=64)
            nc.vector.quantize_mx(out=y_codes[:].bitcast(FP8X4), scales=y_scales[:, cols], in_=y_t[pair][:])
            nc.sync.dma_start(
                out=out_1[0, :, cols, :].rearrange("p m t -> p (m t)").bitcast(I32), in_=y_codes[:].bitcast(I32)
            )

        def store_scales(cols):
            for quad in range(4):
                nc.sync.dma_start(
                    out=out_2[0, 4 * quad : 4 * quad + 4, cols].bitcast(I32),
                    in_=y_scales[32 * quad : 32 * quad + 4, cols].bitcast(I32),
                )

        load_x(0)
        load_x(1)
        load_v_words(0, 1)
        load_x(2)
        load_x(3)
        load_v_scales(0)
        load_v_words(1, 2)
        nc.gpsimd.dma_start(out=gain_raw[0:8, :], in_=range_gain.rearrange("b (h f) -> (b h) f", h=2))
        nc.gpsimd.dma_start(out=gain_raw[32:48, 0:P], in_=row_gain.rearrange("b (j r) -> (b j) r", j=4))
        nc.gpsimd.dma_start(out=gain_raw[64:80, 0:P], in_=col_gain.rearrange("b (j d) -> (b j) d", j=4))
        load_second(0)
        load_x(4)
        load_x(5)
        load_second(1)
        for piece in range(2):
            sort_x(piece)
            turn_x(piece)
        nc.vector.memset(vs_raw[:, 2 * F :].bitcast(I32), 0)
        load_x(6)
        load_x(7)
        for b in range(1, G):
            load_v_words(2 * b, 2 * b + 2)
            load_v_scales(b)
            for h in range(2):
                for piece in range(4 * b + 4 + 2 * h, min(4 * b + 6 + 2 * h, PIECES)):
                    load_x(piece)
                load_second(2 * b + h)

        for piece in range(2, 4):
            sort_x(piece)
            turn_x(piece)
        sort_gains()
        quantize_x(0)
        sort_v(0, 1)
        sort_v(1, 2)
        quantize_x(1)
        for g in range(2):
            for e in range(2):
                filter_pass(e, g)
        for e in range(2):
            limit(e)
        filter_and_limit(2)
        filter_and_limit(3)
        transpose_gains()
        turn_x(4)
        turn_x(5)
        interleave_on_vector(0, 0, HALF, "s_il")
        interleave_on_vector(0, HALF, N, "s_il_gpsimd")
        quantize_second(0, 0, HALF)
        quantize_second(0, HALF, N)

        for a in range(PASSES - 1):
            gpsimd_first = HALF if a == 1 else 0
            x_pieces = X_PIECES_OF_STEP[a]
            early = 2 if a < 2 else 1

            if a >= 2:
                correlate_and_square(2 * a - 4)
                correlate_and_square(2 * a - 3)
            filter_and_limit(4 * a + 4)
            filter_and_limit(4 * a + 5)
            for piece in x_pieces[:early]:
                turn_x(piece)
            if a % 2 == 1:
                spread_col_gain(a // 2)
            filter_and_limit(4 * a + 6)
            filter_and_limit(4 * a + 7)
            for piece in x_pieces[early:]:
                turn_x(piece)
            if a >= 3:
                turn_y(2 * a - 6, 2 * a - 4, nc.scalar.copy, tr_bank())

            interleave_on_gpsimd(a + 1, gpsimd_first, N)
            apply_range_gain(a, 0, R)
            if a >= 2:
                weigh(2 * a - 4)
                weigh(2 * a - 3)
                store_y(2 * a - 4, 2 * a - 2)
                round_y(2 * a - 4, 2 * a - 2, nc.scalar.copy)

            if a == 0:
                quantize_x(2)
            if a == 1:
                interleave_on_vector(2, 0, HALF, "s_il")
            if a % 2 == 0 and a + 2 < PASSES:
                sort_v(a + 2, a + 4)
            if a != 1 and a + 3 < PASSES:
                quantize_x(a + 3)
            quantize_h(a, 0, R)
            if a == 1:
                quantize_second(2, 0, HALF)
                quantize_x(4)
            if a >= 4:
                quantize_y(a - 4)
            quantize_second(a + 1, gpsimd_first, N)

        last_pass = PASSES - 1
        spread_col_gain(G - 1)
        correlate_and_square(10)
        correlate_and_square(11)
        turn_y(8, 10, nc.scalar.copy, tr_bank())
        apply_range_gain(last_pass, 0, HALF)
        quantize_y(3)
        store_scales(slice(0, 2 * R))
        quantize_h(last_pass, 0, HALF)
        correlate_and_square(12)
        correlate_and_square(13)
        apply_range_gain(last_pass, HALF, R)
        weigh(10)
        quantize_h(last_pass, HALF, R)
        quantize_y(4)
        correlate_and_square(14)
        correlate_and_square(15)
        weigh(11)
        store_y(10, 12)
        round_y_on_gpsimd(11)
        round_y(10, 11, nc.scalar.copy)
        weigh(12)
        weigh(13)
        store_y(12, 14)
        round_y(12, 13, nc.scalar.copy)
        round_y_on_gpsimd(13)
        turn_y(10, 12, nc.scalar.copy, tr_bank())
        weigh(14)
        store_y(14, 15)
        weigh(15)
        store_y(15, 16)
        round_y(14, 15, nc.vector.tensor_copy)
        round_y(15, 16, nc.vector.tensor_copy)
        turn_y(12, 14, nc.vector.tensor_copy, tr_bank())
        turn_y(14, 15, nc.scalar.copy, mm_bank())
        turn_y(15, 16, nc.scalar.copy, mm_bank())
        for pair in range(5, 8):
            quantize_y(pair)
        store_scales(slice(2 * R, 4 * R))
